import numpy as np
import ml_dtypes


def mxq(x, axis, fmt="e4m3"):
    dtype, down = {"e4m3": (ml_dtypes.float8_e4m3fn, 7), "e5m2": (ml_dtypes.float8_e5m2, 14)}[fmt]
    v = np.moveaxis(np.asarray(x, np.float32).astype(ml_dtypes.bfloat16).astype(np.float64), axis, -1)
    blocks = v.reshape(v.shape[:-1] + (-1, 32))
    amax = np.abs(blocks).max(-1, keepdims=True)
    byte = np.maximum(np.where(amax > 0, np.frexp(amax)[1] - 1 + 127, 0) - down, 1)
    scale = np.exp2(byte - 127.0)
    codes = (blocks / scale).astype(np.float32).astype(dtype).astype(np.float64)
    return np.moveaxis((codes * scale).reshape(v.shape), -1, axis)


WIDE = False


def mx_kscale(k, group=512):
    if not WIDE:
        return np.ones(k)
    levels = np.array([18, -18])
    if group != 512:
        return np.exp2(np.random.permutation(np.resize(levels, k // group))).repeat(group)
    if k % 512:
        return np.exp2(np.random.permutation(np.resize(levels, k // 32))).repeat(32)
    a = np.empty((k // 512, 16))
    for p in range(k // 512):
        a[p, :8] = np.random.permutation(np.resize(levels, 8))
        for g in range(8):
            far = levels[np.abs(levels - a[p, g]) >= 10]
            a[p, g + 8] = far[np.random.randint(len(far))]
    return np.exp2(a.ravel()).repeat(32)


def f64(x):
    return np.asarray(x).astype(np.float64)


G, D, K, M, N = 4, 128, 512, 128, 512


def setup_inputs():
    n = np.random.standard_normal
    s = mx_kscale(D, 0)[:, None]
    u = mx_kscale(K)[:, None]
    return {
        "x": (n((G, D, N)) * s).astype(np.float32),
        "w1": (n((G, D, K)) / np.sqrt(D) / s).astype(np.float32),
        "hs": (np.random.uniform(0.5, 2.0, (G, K, 1)) * u).astype(np.float32),
        "w2": (n((G, K, M)) / np.sqrt(K) / u).astype(np.float32),
    }


def reference(x, w1, hs, w2):
    xq = mxq(f64(x), 1, "e4m3")
    h = mxq(f64(w1), 1, "e4m3").transpose(0, 2, 1) @ xq
    h = (np.tanh(h)) * f64(hs)
    y = mxq(f64(w2), 1, "e4m3").transpose(0, 2, 1) @ mxq(h, 1, "e4m3")
    return y

@@ -1,0 +1,181 @@
+from contextlib import ExitStack
+
+import concourse.mybir as mybir
+
+G, D, K, M, N = 4, 128, 512, 128, 512
+FLOPS = 2 * G * D * K * N + 2 * G * K * M * N
+
+F32 = mybir.dt.float32
+BF16 = mybir.dt.bfloat16
+U32 = mybir.dt.uint32
+U8 = mybir.dt.uint8
+FP8X4 = mybir.dt.float8_e4m3fn_x4
+ACT = mybir.ActivationFunctionType
+ALU = mybir.AluOpType
+
+P = 128
+CH = 128
+ORDER = "cx0:V qx0:V cw1a:V qa10:V qa11:V qa12:V qa13:V cw1b:V cw1s:A cw1v:V qw10:V qw11:V qw12:V qw13:V cx1:V Z0:P Z1:P qx1:V T0:A cx2:V T1:A M0:V T2:A Z2:P M1:V T3:A qx2:V Q0:V M2:V cw20:A Z3:P Q1:V cx3:V T4:A M3:V T5:A Q2:V qx3:V cw21:A M4:V Z4:P Q3:V T6:A M5:V T7:A Q4:V qw20:V M6:V cw22:A Z5:P Q5:V qw21:V T8:A Y0:P M7:V Y1:P cw23:A Q6:V qw22:V M8:V Y2:P T9:A Q7:V qw23:V T10:A Z6:P M9:V T11:A Q8:V Y3:P M10:V Y4:P Y5:P T12:A Y6:P Q9:V Y7:P M11:V Z7:P T13:A Q10:V O0:A M12:V Y8:P Y9:P Y10:P T14:A Q11:V S0:S M13:V Y11:P O1:A Q12:V M14:V Y12:P T15:A S1:S Q13:V O2:A Y13:P M15:V O3:A S2:S Q14:V Q15:V Y14:P S3:S Y15:P O4:A O5:A S4:S S5:S"
+LOADS = "x0 w1a w1b w1c x1 hs x23 w2a w2b"
+VS = 20
+WARM = True
+
+
+def tile_rows_gmlp_tanh_kernel(tc, x, w1, hs, w2, out):
+    nc = tc.nc
+    with ExitStack() as ctx:
+        sb = ctx.enter_context(tc.tile_pool(name="sb", bufs=1))
+        ps = ctx.enter_context(tc.psum_pool(name="ps", bufs=1))
+        ctx.enter_context(tc.manual_schedule())
+
+        xv = x.flatten_outer_dims().rearrange("(p j) n -> p j n", j=4)
+        w1v = w1.flatten_outer_dims().rearrange("(p j) k -> p j k", j=4)
+        w2v = w2.rearrange("g (p j) m -> p g (j m)", j=4)
+        hsv = hs.rearrange("g (p r) o -> p g (r o)", r=4)
+
+        x0_raw = sb.tile([P, 4, CH], F32, name="x0_raw", align_bytes=64)
+        x1_raw = sb.tile([P, 4, CH], F32, name="x1_raw", align_bytes=64)
+        x23_raw = sb.tile([P, 4, 2 * CH], F32, name="x23_raw", align_bytes=64)
+        x_raw = [x0_raw[:], x1_raw[:], x23_raw[:, :, 0:CH], x23_raw[:, :, CH : 2 * CH]]
+        w1a_raw = sb.tile([P, 4, 256], F32, name="w1a_raw", align_bytes=64)
+        w1b_raw = sb.tile([P, 4, 128], F32, name="w1b_raw", align_bytes=64)
+        w1c_raw = sb.tile([P, 4, 128], F32, name="w1c_raw", align_bytes=64)
+        w2_raw = [sb.tile([P, 2, 512], F32, name="w2_raw%d" % i, align_bytes=64) for i in range(2)]
+        hs_sb = sb.tile([P, G, 8], F32, name="hs_sb", align_bytes=64)
+
+        x_b = [sb.tile([P, CH, 4], BF16, name="x_b%d" % c, align_bytes=64) for c in range(4)]
+        x_q = [sb.tile([P, CH], U32, name="x_q%d" % c, align_bytes=64) for c in range(4)]
+        x_s = [sb.tile([P, CH], U8, name="x_s%d" % c, align_bytes=64) for c in range(4)]
+        w1_b = sb.tile([P, 4, 128, 4], BF16, name="w1_b", align_bytes=64)
+        w1_q = sb.tile([P, 4, 128], U32, name="w1_q", align_bytes=64)
+        w1_s = sb.tile([P, 4, 128], U8, name="w1_s", align_bytes=64)
+        w2_b = [sb.tile([P, M, 4], BF16, name="w2_b%d" % g, align_bytes=64) for g in range(G)]
+        w2_q = [sb.tile([P, M], U32, name="w2_q%d" % g, align_bytes=64) for g in range(G)]
+        w2_s = [sb.tile([P, M], U8, name="w2_s%d" % g, align_bytes=64) for g in range(G)]
+        t_f = [sb.tile([P, CH, 4], F32, name="t_f%d" % u, align_bytes=64) for u in range(16)]
+        h_b = [sb.tile([P, CH, 4], BF16, name="h_b%d" % u, align_bytes=64) for u in range(16)]
+        h_q = [sb.tile([P, CH], U32, name="h_q%d" % u, align_bytes=64) for u in range(16)]
+        h_s = [sb.tile([P, CH], U8, name="h_s%d" % u, align_bytes=64) for u in range(16)]
+        z_ps = [ps.tile([P, 4, CH], F32, name="z_ps%d" % g) for g in range(G)]
+        y_ps = [ps.tile([P, 4, CH], F32, name="y_ps%d" % b) for b in range(4)]
+        pieces = [(0, 0, 4, 0), (1, 0, 4, 1), (2, 0, 4, 2), (3, 0, 2, 3), (3, 2, 1, 0), (3, 3, 1, 1)]
+        y_sb = [sb.tile([P, pc[2], CH], F32, name="y_sb%d" % i, align_bytes=64) for i, pc in enumerate(pieces)]
+
+        loads = {
+            "x0": (x0_raw[:], xv[:, :, 0:128]),
+            "x1": (x1_raw[:], xv[:, :, 128:256]),
+            "x23": (x23_raw[:], xv[:, :, 256:512]),
+            "w1a": (w1a_raw[:], w1v[:, :, 0:256]),
+            "w1b": (w1b_raw[:], w1v[:, :, 256:384]),
+            "w1c": (w1c_raw[:], w1v[:, :, 384:512]),
+            "w2a": (w2_raw[0][:], w2v[:, 0:2, :]),
+            "w2b": (w2_raw[1][:], w2v[:, 2:4, :]),
+            "hs": (hs_sb[:, :, 0:4], hsv),
+        }
+        for name in LOADS.split():
+            nc.sync.dma_start(out=loads[name][0], in_=loads[name][1])
+
+        if WARM:
+            warm = sb.tile([P, 8], F32, name="warm", align_bytes=64)
+            warm_out = sb.tile([P, 8], F32, name="warm_out", align_bytes=64)
+            nc.vector.memset(warm[:], 0.0)
+            nc.scalar.activation(out=warm_out[:], in_=warm[:], func=ACT.Tanh)
+
+        def copy(eng, dst, src):
+            if eng == "V":
+                nc.vector.tensor_copy(out=dst, in_=src)
+            else:
+                nc.scalar.copy(out=dst, in_=src)
+
+        def interleave(eng, dst, src):
+            copy(eng, dst.rearrange("p (c i) j -> p c j i", i=4), src.rearrange("p j (c i) -> p c j i", i=4))
+
+        def deal(eng, s0, raw, a, b):
+            dst = w1_b[:, :, s0 + a : s0 + b, :].rearrange("p r s j -> p s j r")
+            src = raw[:, :, 4 * a : 4 * b].rearrange("p j (s r) -> p s j r", r=4)
+            copy(eng, dst, src)
+
+        def quant(codes, scales, src):
+            nc.vector.quantize_mx(out=codes.bitcast(FP8X4), scales=scales, in_=src)
+
+        def place(u):
+            for i, (c, g0, ng, bank) in enumerate(pieces):
+                if u // 4 == c and g0 <= u % 4 < g0 + ng:
+                    return bank, u % 4 - g0
+            raise ValueError(u)
+
+        for item in ORDER.split():
+            name, eng = item.split(":")
+            if name.startswith("cx"):
+                c = int(name[2:])
+                interleave(eng, x_b[c][:], x_raw[c])
+            elif name.startswith("qx"):
+                c = int(name[2:])
+                quant(x_q[c][:], x_s[c][:], x_b[c][:].rearrange("p n j -> p (n j)"))
+            elif name == "cw1a":
+                deal(eng, 0, w1a_raw, 0, 64)
+            elif name == "cw1b":
+                deal(eng, 64, w1b_raw, 0, 32)
+            elif name == "cw1v":
+                deal(eng, 96, w1c_raw, 0, VS)
+            elif name == "cw1s":
+                deal(eng, 96, w1c_raw, VS, 32)
+            elif name.startswith("qa1") or name.startswith("qw1"):
+                r = int(name[3:])
+                s = slice(0, 64) if name[1] == "a" else slice(64, 128)
+                quant(w1_q[:, r, s], w1_s[:, r, s], w1_b[:, r, s, :].rearrange("p s j -> p (s j)"))
+            elif name.startswith("cw2"):
+                g = int(name[3:])
+                interleave(eng, w2_b[g][:], w2_raw[g // 2][:, g % 2, :].rearrange("p (j m) -> p j m", j=4))
+            elif name.startswith("qw2"):
+                g = int(name[3:])
+                quant(w2_q[g][:], w2_s[g][:], w2_b[g][:].rearrange("p n j -> p (n j)"))
+            elif name[0] == "Z":
+                p = int(name[1:])
+                c = p // 2
+                groups = [0, 1, 2, 3] if p == 0 else ([] if p == 1 else [2 * (p % 2), 2 * (p % 2) + 1])
+                for r in range(4):
+                    for g in groups:
+                        rows = slice(32 * g, 32 * g + 32)
+                        nc.tensor.matmul_mx(
+                            out=z_ps[g][:, r, :],
+                            lhsT=w1_q[rows, r, :].bitcast(FP8X4),
+                            lhsT_scale=w1_s[rows, r, :],
+                            rhs=x_q[c][rows, :].bitcast(FP8X4),
+                            rhs_scale=x_s[c][rows, :],
+                            start=True,
+                            stop=True,
+                        )
+            elif name[0] == "T":
+                u = int(name[1:])
+                nc.scalar.activation(out=t_f[u][:], in_=z_ps[u % 4][:].rearrange("p r n -> p n r"), func=ACT.Tanh)
+            elif name[0] == "M":
+                u = int(name[1:])
+                scale = hs_sb[:, u % 4, 0:4].unsqueeze(1).broadcast_to([P, CH, 4])
+                nc.vector.tensor_tensor(out=h_b[u][:], in0=t_f[u][:], in1=scale, op=ALU.mult)
+            elif name[0] == "Q":
+                u = int(name[1:])
+                quant(h_q[u][:], h_s[u][:], h_b[u][:].rearrange("p n j -> p (n j)"))
+            elif name[0] == "Y":
+                u = int(name[1:])
+                g = u % 4
+                bank, slot = place(u)
+                nc.tensor.matmul_mx(
+                    out=y_ps[bank][:, slot, :],
+                    lhsT=w2_q[g][:].bitcast(FP8X4),
+                    lhsT_scale=w2_s[g][:],
+                    rhs=h_q[u][:].bitcast(FP8X4),
+                    rhs_scale=h_s[u][:],
+                    start=True,
+                    stop=True,
+                )
+            elif name[0] == "O":
+                i = int(name[1:])
+                c, g0, ng, bank = pieces[i]
+                copy(eng, y_sb[i][:], y_ps[bank][:, 0:ng, :])
+            elif name[0] == "S":
+                i = int(name[1:])
+                c, g0, ng, bank = pieces[i]
+                nc.sync.dma_start(
+                    out=out[g0 : g0 + ng, :, c * CH : (c + 1) * CH].rearrange("g m n -> m g n"), in_=y_sb[i][:]
+                )

@@ -14,11 +14,26 @@ ACT = mybir.ActivationFunctionType
 ALU = mybir.AluOpType
 
 P = 128
-CH = 128
-ORDER = "cx0:V qx0:V cw1a:V qa10:V qa11:V qa12:V qa13:V cw1b:V cw1s:A cw1v:V qw10:V qw11:V qw12:V qw13:V cx1:V Z0:P Z1:P qx1:V T0:A cx2:V T1:A M0:V T2:A Z2:P M1:V T3:A qx2:V Q0:V M2:V cw20:A Z3:P Q1:V cx3:V T4:A M3:V T5:A Q2:V qx3:V cw21:A M4:V Z4:P Q3:V T6:A M5:V T7:A Q4:V qw20:V M6:V cw22:A Z5:P Q5:V qw21:V T8:A Y0:P M7:V Y1:P cw23:A Q6:V qw22:V M8:V Y2:P T9:A Q7:V qw23:V T10:A Z6:P M9:V T11:A Q8:V Y3:P M10:V Y4:P Y5:P T12:A Y6:P Q9:V Y7:P M11:V Z7:P T13:A Q10:V O0:A M12:V Y8:P Y9:P Y10:P T14:A Q11:V S0:S M13:V Y11:P O1:A Q12:V M14:V Y12:P T15:A S1:S Q13:V O2:A Y13:P M15:V O3:A S2:S Q14:V Q15:V Y14:P S3:S Y15:P O4:A O5:A S4:S S5:S"
-LOADS = "x0 w1a w1b w1c x1 hs x23 w2a w2b"
-VS = 20
-WARM = True
+PACK = 4
+ROWS = D // PACK
+COLS = 128
+CHUNKS = N // COLS
+UNITS = G * CHUNKS
+HS_PITCH = 8
+ALIGN = 64
+
+DEAL_SPLIT = 80
+SCALAR_PAUSE = 6
+VECTOR_EXTRAS = {
+    2: [("lay_x", 2)],
+    4: [("quant_x", 2)],
+    SCALAR_PAUSE: [("quant_h", 0, 4), ("quant_x", 3), ("quant_w2",)],
+    9: [("quant_h", 4, 4)],
+    12: [("quant_h", 8, 4)],
+    14: [("quant_h", 12, 2)],
+    15: [("quant_h", 14, 1), ("quant_h", 15, 1)],
+}
+PIECES = [(0, 2, 0, 2, 0), (0, 2, 2, 2, 1), (2, 1, 0, 4, 2), (3, 1, 0, 2, 3), (3, 1, 2, 1, 0), (3, 1, 3, 1, 1)]
 
 
 def tile_rows_gmlp_tanh_kernel(tc, x, w1, hs, w2, out):
@@ -28,154 +43,152 @@ def tile_rows_gmlp_tanh_kernel(tc, x, w1, hs, w2, out):
         ps = ctx.enter_context(tc.psum_pool(name="ps", bufs=1))
         ctx.enter_context(tc.manual_schedule())
 
-        xv = x.flatten_outer_dims().rearrange("(p j) n -> p j n", j=4)
-        w1v = w1.flatten_outer_dims().rearrange("(p j) k -> p j k", j=4)
-        w2v = w2.rearrange("g (p j) m -> p g (j m)", j=4)
-        hsv = hs.rearrange("g (p r) o -> p g (r o)", r=4)
+        def sbuf(name, shape, dtype):
+            return sb.tile([P] + shape, dtype, name=name, align_bytes=ALIGN)
 
-        x0_raw = sb.tile([P, 4, CH], F32, name="x0_raw", align_bytes=64)
-        x1_raw = sb.tile([P, 4, CH], F32, name="x1_raw", align_bytes=64)
-        x23_raw = sb.tile([P, 4, 2 * CH], F32, name="x23_raw", align_bytes=64)
-        x_raw = [x0_raw[:], x1_raw[:], x23_raw[:, :, 0:CH], x23_raw[:, :, CH : 2 * CH]]
-        w1a_raw = sb.tile([P, 4, 256], F32, name="w1a_raw", align_bytes=64)
-        w1b_raw = sb.tile([P, 4, 128], F32, name="w1b_raw", align_bytes=64)
-        w1c_raw = sb.tile([P, 4, 128], F32, name="w1c_raw", align_bytes=64)
-        w2_raw = [sb.tile([P, 2, 512], F32, name="w2_raw%d" % i, align_bytes=64) for i in range(2)]
-        hs_sb = sb.tile([P, G, 8], F32, name="hs_sb", align_bytes=64)
+        w1_raw = sbuf("w1_raw", [PACK, K], F32)
+        x0_raw = sbuf("x0_raw", [PACK, COLS], F32)
+        x1_raw = sbuf("x1_raw", [PACK, COLS], F32)
+        x23_raw = sbuf("x23_raw", [PACK, 2 * COLS], F32)
+        x_raw = [x0_raw[:], x1_raw[:], x23_raw[:, :, 0:COLS], x23_raw[:, :, COLS : 2 * COLS]]
+        w2_raw = sbuf("w2_raw", [G, PACK * M], F32)
+        hs_sb = sbuf("hs_sb", [G, HS_PITCH], F32)
+        x_bf = [sbuf("x_bf%d" % c, [COLS, PACK], BF16) for c in range(CHUNKS)]
+        x_codes = [sbuf("x_codes%d" % c, [COLS], U32) for c in range(CHUNKS)]
+        x_scales = [sbuf("x_scales%d" % c, [COLS], U8) for c in range(CHUNKS)]
+        w1_bf = sbuf("w1_bf", [PACK, P, PACK], BF16)
+        w1_codes = sbuf("w1_codes", [PACK, P], U32)
+        w1_scales = sbuf("w1_scales", [PACK, P], U8)
+        w2_bf = sbuf("w2_bf", [G, M, PACK], BF16)
+        w2_codes = sbuf("w2_codes", [G, M], U32)
+        w2_scales = sbuf("w2_scales", [G, M], U8)
+        tanh_z = sbuf("tanh_z", [UNITS, COLS, PACK], F32)
+        h_bf = sbuf("h_bf", [UNITS, COLS, PACK], BF16)
+        h_codes = sbuf("h_codes", [UNITS, COLS], U32)
+        h_scales = sbuf("h_scales", [UNITS, COLS], U8)
+        y_sb = [sbuf("y_sb%d" % i, [piece[3], piece[1] * COLS], F32) for i, piece in enumerate(PIECES)]
+        z_ps = [ps.tile([P, PACK, COLS], F32, name="z_ps%d" % g) for g in range(G)]
+        y_ps = [ps.tile([P, PACK, COLS], F32, name="y_ps%d" % b) for b in range(4)]
 
-        x_b = [sb.tile([P, CH, 4], BF16, name="x_b%d" % c, align_bytes=64) for c in range(4)]
-        x_q = [sb.tile([P, CH], U32, name="x_q%d" % c, align_bytes=64) for c in range(4)]
-        x_s = [sb.tile([P, CH], U8, name="x_s%d" % c, align_bytes=64) for c in range(4)]
-        w1_b = sb.tile([P, 4, 128, 4], BF16, name="w1_b", align_bytes=64)
-        w1_q = sb.tile([P, 4, 128], U32, name="w1_q", align_bytes=64)
-        w1_s = sb.tile([P, 4, 128], U8, name="w1_s", align_bytes=64)
-        w2_b = [sb.tile([P, M, 4], BF16, name="w2_b%d" % g, align_bytes=64) for g in range(G)]
-        w2_q = [sb.tile([P, M], U32, name="w2_q%d" % g, align_bytes=64) for g in range(G)]
-        w2_s = [sb.tile([P, M], U8, name="w2_s%d" % g, align_bytes=64) for g in range(G)]
-        t_f = [sb.tile([P, CH, 4], F32, name="t_f%d" % u, align_bytes=64) for u in range(16)]
-        h_b = [sb.tile([P, CH, 4], BF16, name="h_b%d" % u, align_bytes=64) for u in range(16)]
-        h_q = [sb.tile([P, CH], U32, name="h_q%d" % u, align_bytes=64) for u in range(16)]
-        h_s = [sb.tile([P, CH], U8, name="h_s%d" % u, align_bytes=64) for u in range(16)]
-        z_ps = [ps.tile([P, 4, CH], F32, name="z_ps%d" % g) for g in range(G)]
-        y_ps = [ps.tile([P, 4, CH], F32, name="y_ps%d" % b) for b in range(4)]
-        pieces = [(0, 0, 4, 0), (1, 0, 4, 1), (2, 0, 4, 2), (3, 0, 2, 3), (3, 2, 1, 0), (3, 3, 1, 1)]
-        y_sb = [sb.tile([P, pc[2], CH], F32, name="y_sb%d" % i, align_bytes=64) for i, pc in enumerate(pieces)]
+        x_hbm = x.flatten_outer_dims().rearrange("(p j) n -> p j n", j=PACK)
+        w1_hbm = w1.flatten_outer_dims().rearrange("(p j) k -> p j k", j=PACK)
+        w2_hbm = w2.rearrange("g (s r) m -> s g (r m)", r=PACK)
+        nc.sync.dma_start(out=w1_raw[:], in_=w1_hbm)
+        nc.sync.dma_start(out=x0_raw[:], in_=x_hbm[:, :, 0:COLS])
+        nc.sync.dma_start(out=x1_raw[:], in_=x_hbm[:, :, COLS : 2 * COLS])
+        for g in range(G - 1):
+            nc.sync.dma_start(out=w2_raw[:, g, :], in_=w2_hbm[:, g, :])
+        nc.sync.dma_start(out=hs_sb[:, :, 0:PACK], in_=hs.rearrange("g (s r) o -> s g (r o)", r=PACK))
+        nc.sync.dma_start(out=x23_raw[:], in_=x_hbm[:, :, 2 * COLS : N])
+        nc.sync.dma_start(out=w2_raw[:, G - 1, :], in_=w2_hbm[:, G - 1, :])
 
-        loads = {
-            "x0": (x0_raw[:], xv[:, :, 0:128]),
-            "x1": (x1_raw[:], xv[:, :, 128:256]),
-            "x23": (x23_raw[:], xv[:, :, 256:512]),
-            "w1a": (w1a_raw[:], w1v[:, :, 0:256]),
-            "w1b": (w1b_raw[:], w1v[:, :, 256:384]),
-            "w1c": (w1c_raw[:], w1v[:, :, 384:512]),
-            "w2a": (w2_raw[0][:], w2v[:, 0:2, :]),
-            "w2b": (w2_raw[1][:], w2v[:, 2:4, :]),
-            "hs": (hs_sb[:, :, 0:4], hsv),
-        }
-        for name in LOADS.split():
-            nc.sync.dma_start(out=loads[name][0], in_=loads[name][1])
+        def lay(copy, dst, src):
+            copy(out=dst.rearrange("p (c i) j -> p c j i", i=4), in_=src.rearrange("p j (c i) -> p c j i", i=4))
 
-        if WARM:
-            warm = sb.tile([P, 8], F32, name="warm", align_bytes=64)
-            warm_out = sb.tile([P, 8], F32, name="warm_out", align_bytes=64)
-            nc.vector.memset(warm[:], 0.0)
-            nc.scalar.activation(out=warm_out[:], in_=warm[:], func=ACT.Tanh)
+        def lay_x(c, copy=nc.vector.tensor_copy):
+            lay(copy, x_bf[c][:], x_raw[c])
 
-        def copy(eng, dst, src):
-            if eng == "V":
-                nc.vector.tensor_copy(out=dst, in_=src)
-            else:
-                nc.scalar.copy(out=dst, in_=src)
+        def lay_w2(g, copy=nc.vector.tensor_copy):
+            lay(copy, w2_bf[:, g, :, :], w2_raw[:, g, :].rearrange("s (r m) -> s r m", r=PACK))
 
-        def interleave(eng, dst, src):
-            copy(eng, dst.rearrange("p (c i) j -> p c j i", i=4), src.rearrange("p j (c i) -> p c j i", i=4))
+        def dealt(s0, s1):
+            dst = w1_bf[:, :, s0:s1, :].rearrange("p r s j -> p s j r")
+            src = w1_raw[:, :, PACK * s0 : PACK * s1].rearrange("p j (s r) -> p s j r", r=PACK)
+            return dst, src
 
-        def deal(eng, s0, raw, a, b):
-            dst = w1_b[:, :, s0 + a : s0 + b, :].rearrange("p r s j -> p s j r")
-            src = raw[:, :, 4 * a : 4 * b].rearrange("p j (s r) -> p s j r", r=4)
-            copy(eng, dst, src)
+        def quant(codes, scales, values):
+            nc.vector.quantize_mx(out=codes.bitcast(FP8X4), scales=scales, in_=values)
 
-        def quant(codes, scales, src):
-            nc.vector.quantize_mx(out=codes.bitcast(FP8X4), scales=scales, in_=src)
+        def quant_x(c):
+            quant(x_codes[c][:], x_scales[c][:], x_bf[c][:].rearrange("p n j -> p (n j)"))
 
-        def place(u):
-            for i, (c, g0, ng, bank) in enumerate(pieces):
-                if u // 4 == c and g0 <= u % 4 < g0 + ng:
-                    return bank, u % 4 - g0
-            raise ValueError(u)
+        def quant_w1(r):
+            quant(w1_codes[:, r, :], w1_scales[:, r, :], w1_bf[:, r, :, :].rearrange("p s j -> p (s j)"))
 
-        for item in ORDER.split():
-            name, eng = item.split(":")
-            if name.startswith("cx"):
-                c = int(name[2:])
-                interleave(eng, x_b[c][:], x_raw[c])
-            elif name.startswith("qx"):
-                c = int(name[2:])
-                quant(x_q[c][:], x_s[c][:], x_b[c][:].rearrange("p n j -> p (n j)"))
-            elif name == "cw1a":
-                deal(eng, 0, w1a_raw, 0, 64)
-            elif name == "cw1b":
-                deal(eng, 64, w1b_raw, 0, 32)
-            elif name == "cw1v":
-                deal(eng, 96, w1c_raw, 0, VS)
-            elif name == "cw1s":
-                deal(eng, 96, w1c_raw, VS, 32)
-            elif name.startswith("qa1") or name.startswith("qw1"):
-                r = int(name[3:])
-                s = slice(0, 64) if name[1] == "a" else slice(64, 128)
-                quant(w1_q[:, r, s], w1_s[:, r, s], w1_b[:, r, s, :].rearrange("p s j -> p (s j)"))
-            elif name.startswith("cw2"):
-                g = int(name[3:])
-                interleave(eng, w2_b[g][:], w2_raw[g // 2][:, g % 2, :].rearrange("p (j m) -> p j m", j=4))
-            elif name.startswith("qw2"):
-                g = int(name[3:])
-                quant(w2_q[g][:], w2_s[g][:], w2_b[g][:].rearrange("p n j -> p (n j)"))
-            elif name[0] == "Z":
-                p = int(name[1:])
-                c = p // 2
-                groups = [0, 1, 2, 3] if p == 0 else ([] if p == 1 else [2 * (p % 2), 2 * (p % 2) + 1])
-                for r in range(4):
-                    for g in groups:
-                        rows = slice(32 * g, 32 * g + 32)
-                        nc.tensor.matmul_mx(
-                            out=z_ps[g][:, r, :],
-                            lhsT=w1_q[rows, r, :].bitcast(FP8X4),
-                            lhsT_scale=w1_s[rows, r, :],
-                            rhs=x_q[c][rows, :].bitcast(FP8X4),
-                            rhs_scale=x_s[c][rows, :],
-                            start=True,
-                            stop=True,
-                        )
-            elif name[0] == "T":
-                u = int(name[1:])
-                nc.scalar.activation(out=t_f[u][:], in_=z_ps[u % 4][:].rearrange("p r n -> p n r"), func=ACT.Tanh)
-            elif name[0] == "M":
-                u = int(name[1:])
-                scale = hs_sb[:, u % 4, 0:4].unsqueeze(1).broadcast_to([P, CH, 4])
-                nc.vector.tensor_tensor(out=h_b[u][:], in0=t_f[u][:], in1=scale, op=ALU.mult)
-            elif name[0] == "Q":
-                u = int(name[1:])
-                quant(h_q[u][:], h_s[u][:], h_b[u][:].rearrange("p n j -> p (n j)"))
-            elif name[0] == "Y":
-                u = int(name[1:])
-                g = u % 4
-                bank, slot = place(u)
-                nc.tensor.matmul_mx(
-                    out=y_ps[bank][:, slot, :],
-                    lhsT=w2_q[g][:].bitcast(FP8X4),
-                    lhsT_scale=w2_s[g][:],
-                    rhs=h_q[u][:].bitcast(FP8X4),
-                    rhs_scale=h_s[u][:],
-                    start=True,
-                    stop=True,
-                )
-            elif name[0] == "O":
-                i = int(name[1:])
-                c, g0, ng, bank = pieces[i]
-                copy(eng, y_sb[i][:], y_ps[bank][:, 0:ng, :])
-            elif name[0] == "S":
-                i = int(name[1:])
-                c, g0, ng, bank = pieces[i]
-                nc.sync.dma_start(
-                    out=out[g0 : g0 + ng, :, c * CH : (c + 1) * CH].rearrange("g m n -> m g n"), in_=y_sb[i][:]
-                )
+        def quant_w2():
+            quant(
+                w2_codes[:].rearrange("s g m -> s (g m)"),
+                w2_scales[:].rearrange("s g m -> s (g m)"),
+                w2_bf[:].rearrange("s g m r -> s (g m r)"),
+            )
+
+        def quant_h(first, count):
+            units = slice(first, first + count)
+            quant(
+                h_codes[:, units, :].rearrange("s u n -> s (u n)"),
+                h_scales[:, units, :].rearrange("s u n -> s (u n)"),
+                h_bf[:, units, :, :].rearrange("s u n r -> s (u n r)"),
+            )
+
+        def first_layer(u, r):
+            c, g = divmod(u, G)
+            rows = slice(ROWS * g, ROWS * (g + 1))
+            nc.tensor.matmul_mx(
+                out=z_ps[g][:, r, :],
+                lhsT=w1_codes[rows, r, :].bitcast(FP8X4),
+                lhsT_scale=w1_scales[rows, r, :],
+                rhs=x_codes[c][rows, :].bitcast(FP8X4),
+                rhs_scale=x_scales[c][rows, :],
+                start=True,
+                stop=True,
+            )
+
+        def second_layer(u, dst):
+            g = u % G
+            nc.tensor.matmul_mx(
+                out=dst,
+                lhsT=w2_codes[:, g, :].bitcast(FP8X4),
+                lhsT_scale=w2_scales[:, g, :],
+                rhs=h_codes[:, u, :].bitcast(FP8X4),
+                rhs_scale=h_scales[:, u, :],
+                start=True,
+                stop=True,
+            )
+
+        vector_jobs = {"lay_x": lay_x, "quant_x": quant_x, "quant_h": quant_h, "quant_w2": quant_w2}
+
+        dst, src = dealt(0, DEAL_SPLIT)
+        nc.vector.tensor_copy(out=dst, in_=src)
+        dst, src = dealt(DEAL_SPLIT, P)
+        nc.scalar.activation(out=dst, in_=src, func=ACT.Copy)
+        lay_x(0)
+        quant_w1(0)
+        quant_x(0)
+        for r in range(1, PACK):
+            quant_w1(r)
+        lay_x(1, nc.scalar.copy)
+        lay_w2(0)
+        lay_w2(1)
+        quant_x(1)
+        lay_w2(2)
+
+        for i in range(UNITS + 2):
+            for r in range(2):
+                if i < UNITS:
+                    first_layer(i, r)
+                if 1 <= i <= UNITS:
+                    first_layer(i - 1, r + 2)
+            u = i - 1
+            if 0 <= u < UNITS:
+                bank_as_words = z_ps[u % G][:].rearrange("s r n -> s n r")
+                nc.scalar.activation(out=tanh_z[:, u, :, :], in_=bank_as_words, func=ACT.Tanh)
+                if u == SCALAR_PAUSE:
+                    lay_w2(G - 1, nc.scalar.copy)
+                    lay_x(CHUNKS - 1, nc.scalar.copy)
+            u = i - 2
+            if u >= 0:
+                scale = hs_sb[:, u % G, 0:PACK].unsqueeze(1).broadcast_to([P, COLS, PACK])
+                nc.vector.tensor_tensor(out=h_bf[:, u, :, :], in0=tanh_z[:, u, :, :], in1=scale, op=ALU.mult)
+                for job in VECTOR_EXTRAS.get(u, []):
+                    vector_jobs[job[0]](*job[1:])
+
+        for i, (c0, chunks, g0, groups, bank) in enumerate(PIECES):
+            for c in range(chunks):
+                for g in range(groups):
+                    second_layer(G * (c0 + c) + g0 + g, y_ps[bank][:, g * chunks + c, :])
+            nc.scalar.copy(
+                out=y_sb[i][:].rearrange("m g n -> m (g n)"),
+                in_=y_ps[bank][:, 0 : groups * chunks, :].rearrange("m a n -> m (a n)"),
+            )
+            out_piece = out[g0 : g0 + groups, :, c0 * COLS : (c0 + chunks) * COLS]
+            nc.sync.dma_start(out=out_piece.rearrange("g m n -> m g n"), in_=y_sb[i][:])

@@ -22,13 +22,15 @@ UNITS = G * CHUNKS
 HS_PITCH = 8
 ALIGN = 64
 
-DEAL_SPLIT = 80
-SCALAR_PAUSE = 6
+W1_SPLIT = 80
+X0_SPLIT = 96
+SCALAR_EXTRAS = {3: ("lay_x", 3), 8: ("lay_w2", 2), 9: ("lay_w2", 3)}
 VECTOR_EXTRAS = {
     2: [("lay_x", 2)],
-    4: [("quant_x", 2)],
-    SCALAR_PAUSE: [("quant_h", 0, 4), ("quant_x", 3), ("quant_w2",)],
-    9: [("quant_h", 4, 4)],
+    3: [("quant_x", 2), ("quant_x", 3)],
+    5: [("quant_h", 0, 4)],
+    8: [("quant_h", 4, 4)],
+    9: [("quant_w2", 2, 2)],
     12: [("quant_h", 8, 4)],
     14: [("quant_h", 12, 2)],
     15: [("quant_h", 14, 1), ("quant_h", 15, 1)],
@@ -76,19 +78,19 @@ def tile_rows_gmlp_tanh_kernel(tc, x, w1, hs, w2, out):
         nc.sync.dma_start(out=w1_raw[:], in_=w1_hbm)
         nc.sync.dma_start(out=x0_raw[:], in_=x_hbm[:, :, 0:COLS])
         nc.sync.dma_start(out=x1_raw[:], in_=x_hbm[:, :, COLS : 2 * COLS])
-        for g in range(G - 1):
+        for g in range(2):
             nc.sync.dma_start(out=w2_raw[:, g, :], in_=w2_hbm[:, g, :])
         nc.sync.dma_start(out=hs_sb[:, :, 0:PACK], in_=hs.rearrange("g (s r) o -> s g (r o)", r=PACK))
         nc.sync.dma_start(out=x23_raw[:], in_=x_hbm[:, :, 2 * COLS : N])
-        nc.sync.dma_start(out=w2_raw[:, G - 1, :], in_=w2_hbm[:, G - 1, :])
+        nc.sync.dma_start(out=w2_raw[:, 2:G, :], in_=w2_hbm[:, 2:G, :])
 
         def lay(copy, dst, src):
             copy(out=dst.rearrange("p (c i) j -> p c j i", i=4), in_=src.rearrange("p j (c i) -> p c j i", i=4))
 
-        def lay_x(c, copy=nc.vector.tensor_copy):
-            lay(copy, x_bf[c][:], x_raw[c])
+        def lay_x(copy, c, n0=0, n1=COLS):
+            lay(copy, x_bf[c][:, n0:n1, :], x_raw[c][:, :, n0:n1])
 
-        def lay_w2(g, copy=nc.vector.tensor_copy):
+        def lay_w2(copy, g):
             lay(copy, w2_bf[:, g, :, :], w2_raw[:, g, :].rearrange("s (r m) -> s r m", r=PACK))
 
         def dealt(s0, s1):
@@ -105,11 +107,12 @@ def tile_rows_gmlp_tanh_kernel(tc, x, w1, hs, w2, out):
         def quant_w1(r):
             quant(w1_codes[:, r, :], w1_scales[:, r, :], w1_bf[:, r, :, :].rearrange("p s j -> p (s j)"))
 
-        def quant_w2():
+        def quant_w2(first, count):
+            groups = slice(first, first + count)
             quant(
-                w2_codes[:].rearrange("s g m -> s (g m)"),
-                w2_scales[:].rearrange("s g m -> s (g m)"),
-                w2_bf[:].rearrange("s g m r -> s (g m r)"),
+                w2_codes[:, groups, :].rearrange("s g m -> s (g m)"),
+                w2_scales[:, groups, :].rearrange("s g m -> s (g m)"),
+                w2_bf[:, groups, :, :].rearrange("s g m r -> s (g m r)"),
             )
 
         def quant_h(first, count):
@@ -145,42 +148,43 @@ def tile_rows_gmlp_tanh_kernel(tc, x, w1, hs, w2, out):
                 stop=True,
             )
 
-        vector_jobs = {"lay_x": lay_x, "quant_x": quant_x, "quant_h": quant_h, "quant_w2": quant_w2}
+        on_vector, on_scalar = nc.vector.tensor_copy, nc.scalar.copy
+        scalar_jobs = {"lay_x": lay_x, "lay_w2": lay_w2}
+        vector_jobs = {
+            "lay_x": lambda c: lay_x(on_vector, c),
+            "quant_x": quant_x,
+            "quant_h": quant_h,
+            "quant_w2": quant_w2,
+        }
 
-        dst, src = dealt(0, DEAL_SPLIT)
+        dst, src = dealt(0, W1_SPLIT)
         nc.vector.tensor_copy(out=dst, in_=src)
-        dst, src = dealt(DEAL_SPLIT, P)
+        dst, src = dealt(W1_SPLIT, P)
         nc.scalar.activation(out=dst, in_=src, func=ACT.Copy)
-        lay_x(0)
+        lay_x(on_vector, 0, 0, X0_SPLIT)
+        lay_x(on_scalar, 0, X0_SPLIT, COLS)
         quant_w1(0)
         quant_x(0)
         for r in range(1, PACK):
             quant_w1(r)
-        lay_x(1, nc.scalar.copy)
-        lay_w2(0)
-        lay_w2(1)
+        lay_x(on_scalar, 1)
+        lay_w2(on_vector, 0)
+        lay_w2(on_vector, 1)
         quant_x(1)
-        lay_w2(2)
+        quant_w2(0, 2)
 
-        for i in range(UNITS + 2):
-            for r in range(2):
-                if i < UNITS:
-                    first_layer(i, r)
-                if 1 <= i <= UNITS:
-                    first_layer(i - 1, r + 2)
-            u = i - 1
-            if 0 <= u < UNITS:
-                bank_as_words = z_ps[u % G][:].rearrange("s r n -> s n r")
-                nc.scalar.activation(out=tanh_z[:, u, :, :], in_=bank_as_words, func=ACT.Tanh)
-                if u == SCALAR_PAUSE:
-                    lay_w2(G - 1, nc.scalar.copy)
-                    lay_x(CHUNKS - 1, nc.scalar.copy)
-            u = i - 2
-            if u >= 0:
-                scale = hs_sb[:, u % G, 0:PACK].unsqueeze(1).broadcast_to([P, COLS, PACK])
-                nc.vector.tensor_tensor(out=h_bf[:, u, :, :], in0=tanh_z[:, u, :, :], in1=scale, op=ALU.mult)
-                for job in VECTOR_EXTRAS.get(u, []):
-                    vector_jobs[job[0]](*job[1:])
+        for u in range(UNITS):
+            g = u % G
+            for r in range(PACK):
+                first_layer(u, r)
+            nc.scalar.activation(out=tanh_z[:, u, :, :], in_=z_ps[g][:].rearrange("s r n -> s n r"), func=ACT.Tanh)
+            if u in SCALAR_EXTRAS:
+                job, index = SCALAR_EXTRAS[u]
+                scalar_jobs[job](on_scalar, index)
+            scale = hs_sb[:, g, 0:PACK].unsqueeze(1).broadcast_to([P, COLS, PACK])
+            nc.vector.tensor_tensor(out=h_bf[:, u, :, :], in0=tanh_z[:, u, :, :], in1=scale, op=ALU.mult)
+            for job in VECTOR_EXTRAS.get(u, []):
+                vector_jobs[job[0]](*job[1:])
 
         for i, (c0, chunks, g0, groups, bank) in enumerate(PIECES):
             for c in range(chunks):

@@ -24,18 +24,38 @@ ALIGN = 64
 
 W1_SPLIT = 80
 X0_SPLIT = 96
-SCALAR_EXTRAS = {3: ("lay_x", 3), 8: ("lay_w2", 2), 9: ("lay_w2", 3)}
-VECTOR_EXTRAS = {
-    2: [("lay_x", 2)],
-    3: [("quant_x", 2), ("quant_x", 3)],
-    5: [("quant_h", 0, 4)],
-    8: [("quant_h", 4, 4)],
-    9: [("quant_w2", 2, 2)],
-    12: [("quant_h", 8, 4)],
-    14: [("quant_h", 12, 2)],
-    15: [("quant_h", 14, 1), ("quant_h", 15, 1)],
+ORDER = [(0,0), (0,1), (0,2), (0,3), (1,0), (1,1), (1,2), (1,3), (2,0), (2,1), (2,2), (2,3), (3,0), (3,1), (3,2), (3,3)]
+HALVED = [15]
+LOADS = [("w1",), ("x",0,1,), ("w2",0,1,), ("w2",1,1,), ("x",1,1,), ("hs",0,4,), ("x",2,2,), ("w2",2,2,)]
+HEAD = [("lay_x","V",0,0,96,), ("lay_x","S",0,96,128,), ("quant_w1",0,), ("quant_x",0,), ("quant_w1",1,), ("quant_w1",2,), ("quant_w1",3,), ("lay_w2","S",0,), ("lay_w2","S",1,), ("quant_w2",0,1,), ("lay_x","V",1,), ("quant_w2",1,1,), ("quant_x",1,), ("mm1",0,), ("mm1",1,), ("mm1",2,), ("mm1",3,)]
+AFTER_TANH = {
+    0: [("mm1",4,)],
+    1: [("mm1",5,)],
+    2: [("mm1",6,)],
+    3: [("mm1",7,), ("lay_x","S",3,)],
+    4: [("mm1",8,)],
+    5: [("mm1",9,)],
+    6: [("mm1",10,)],
+    7: [("mm1",11,)],
+    8: [("mm1",12,), ("lay_w2","S",2,)],
+    9: [("mm1",13,), ("mm2",0,), ("lay_w2","S",3,)],
+    10: [("mm1",14,), ("mm2",1,)],
+    11: [("mm1",15,)],
+    12: [("out","S",0,)],
+    14: [("out","S",1,)],
 }
-PIECES = [(0, 2, 0, 2, 0), (0, 2, 2, 2, 1), (2, 1, 0, 4, 2), (3, 1, 0, 2, 3), (3, 1, 2, 1, 0), (3, 1, 3, 1, 1)]
+AFTER_MULT = {
+    2: [("mult",2,), ("lay_x","V",2,)],
+    3: [("mult",3,), ("quant_x",2,), ("quant_x",3,)],
+    5: [("mult",5,), ("quant_h",0,4,)],
+    8: [("mult",8,), ("quant_h",4,4,)],
+    9: [("mult",9,), ("quant_w2",2,2,)],
+    12: [("mult",12,), ("quant_h",8,4,)],
+    14: [("mult",14,), ("quant_h",12,2,)],
+    15: [("mult_half",15,0,), ("mult_half",15,1,), ("quant_h",14,1,), ("quant_h",15,1,)],
+}
+TAIL = [("mm2",2,), ("out","S",2,), ("mm2",3,), ("out","S",3,), ("mm2",4,), ("out","S",4,), ("mm2",5,), ("out","S",5,), ("mm2",6,), ("out","V",6,)]
+PIECES = [(0,2,0,2,0,), (0,2,2,2,1,), (2,1,0,2,2,), (2,1,2,2,3,), (3,1,0,2,0,), (3,1,2,1,1,), (3,1,3,1,2,)]
 
 
 def tile_rows_gmlp_tanh_kernel(tc, x, w1, hs, w2, out):
@@ -48,13 +68,13 @@ def tile_rows_gmlp_tanh_kernel(tc, x, w1, hs, w2, out):
         def sbuf(name, shape, dtype):
             return sb.tile([P] + shape, dtype, name=name, align_bytes=ALIGN)
 
+        x_hbm = x.flatten_outer_dims().rearrange("(p j) n -> p j n", j=PACK)
+        w1_hbm = w1.flatten_outer_dims().rearrange("(p j) k -> p j k", j=PACK)
+        w2_hbm = w2.rearrange("g (s r) m -> s g (r m)", r=PACK)
         w1_raw = sbuf("w1_raw", [PACK, K], F32)
-        x0_raw = sbuf("x0_raw", [PACK, COLS], F32)
-        x1_raw = sbuf("x1_raw", [PACK, COLS], F32)
-        x23_raw = sbuf("x23_raw", [PACK, 2 * COLS], F32)
-        x_raw = [x0_raw[:], x1_raw[:], x23_raw[:, :, 0:COLS], x23_raw[:, :, COLS : 2 * COLS]]
         w2_raw = sbuf("w2_raw", [G, PACK * M], F32)
         hs_sb = sbuf("hs_sb", [G, HS_PITCH], F32)
+        x_raw = {}
         x_bf = [sbuf("x_bf%d" % c, [COLS, PACK], BF16) for c in range(CHUNKS)]
         x_codes = [sbuf("x_codes%d" % c, [COLS], U32) for c in range(CHUNKS)]
         x_scales = [sbuf("x_scales%d" % c, [COLS], U8) for c in range(CHUNKS)]
@@ -72,17 +92,21 @@ def tile_rows_gmlp_tanh_kernel(tc, x, w1, hs, w2, out):
         z_ps = [ps.tile([P, PACK, COLS], F32, name="z_ps%d" % g) for g in range(G)]
         y_ps = [ps.tile([P, PACK, COLS], F32, name="y_ps%d" % b) for b in range(4)]
 
-        x_hbm = x.flatten_outer_dims().rearrange("(p j) n -> p j n", j=PACK)
-        w1_hbm = w1.flatten_outer_dims().rearrange("(p j) k -> p j k", j=PACK)
-        w2_hbm = w2.rearrange("g (s r) m -> s g (r m)", r=PACK)
-        nc.sync.dma_start(out=w1_raw[:], in_=w1_hbm)
-        nc.sync.dma_start(out=x0_raw[:], in_=x_hbm[:, :, 0:COLS])
-        nc.sync.dma_start(out=x1_raw[:], in_=x_hbm[:, :, COLS : 2 * COLS])
-        for g in range(2):
-            nc.sync.dma_start(out=w2_raw[:, g, :], in_=w2_hbm[:, g, :])
-        nc.sync.dma_start(out=hs_sb[:, :, 0:PACK], in_=hs.rearrange("g (s r) o -> s g (r o)", r=PACK))
-        nc.sync.dma_start(out=x23_raw[:], in_=x_hbm[:, :, 2 * COLS : N])
-        nc.sync.dma_start(out=w2_raw[:, 2:G, :], in_=w2_hbm[:, 2:G, :])
+        for load in LOADS:
+            if load[0] == "w1":
+                nc.sync.dma_start(out=w1_raw[:], in_=w1_hbm)
+            elif load[0] == "x":
+                first, count = load[1:]
+                raw = sbuf("x_raw%d" % first, [PACK, count * COLS], F32)
+                nc.sync.dma_start(out=raw[:], in_=x_hbm[:, :, first * COLS : (first + count) * COLS])
+                for c in range(count):
+                    x_raw[first + c] = raw[:, :, c * COLS : (c + 1) * COLS]
+            elif load[0] == "w2":
+                groups = slice(load[1], load[1] + load[2])
+                nc.sync.dma_start(out=w2_raw[:, groups, :], in_=w2_hbm[:, groups, :])
+            else:
+                groups = slice(load[1], load[1] + load[2])
+                nc.sync.dma_start(out=hs_sb[:, groups, 0:PACK], in_=hs.rearrange("g (s r) o -> s g (r o)", r=PACK)[:, groups, :])
 
         def lay(copy, dst, src):
             copy(out=dst.rearrange("p (c i) j -> p c j i", i=4), in_=src.rearrange("p j (c i) -> p c j i", i=4))
@@ -90,8 +114,8 @@ def tile_rows_gmlp_tanh_kernel(tc, x, w1, hs, w2, out):
         def lay_x(copy, c, n0=0, n1=COLS):
             lay(copy, x_bf[c][:, n0:n1, :], x_raw[c][:, :, n0:n1])
 
-        def lay_w2(copy, g):
-            lay(copy, w2_bf[:, g, :, :], w2_raw[:, g, :].rearrange("s (r m) -> s r m", r=PACK))
+        def lay_w2(copy, g, m0=0, m1=M):
+            lay(copy, w2_bf[:, g, m0:m1, :], w2_raw[:, g, :].rearrange("s (r m) -> s r m", r=PACK)[:, :, m0:m1])
 
         def dealt(s0, s1):
             dst = w1_bf[:, :, s0:s1, :].rearrange("p r s j -> p s j r")
@@ -104,8 +128,9 @@ def tile_rows_gmlp_tanh_kernel(tc, x, w1, hs, w2, out):
         def quant_x(c):
             quant(x_codes[c][:], x_scales[c][:], x_bf[c][:].rearrange("p n j -> p (n j)"))
 
-        def quant_w1(r):
-            quant(w1_codes[:, r, :], w1_scales[:, r, :], w1_bf[:, r, :, :].rearrange("p s j -> p (s j)"))
+        def quant_w1(r, count=1):
+            rs = slice(r, r + count)
+            quant(w1_codes[:, rs, :].rearrange("p r s -> p (r s)"), w1_scales[:, rs, :].rearrange("p r s -> p (r s)"), w1_bf[:, rs, :, :].rearrange("p r s j -> p (r s j)"))
 
         def quant_w2(first, count):
             groups = slice(first, first + count)
@@ -124,7 +149,7 @@ def tile_rows_gmlp_tanh_kernel(tc, x, w1, hs, w2, out):
             )
 
         def first_layer(u, r):
-            c, g = divmod(u, G)
+            c, g = ORDER[u]
             rows = slice(ROWS * g, ROWS * (g + 1))
             nc.tensor.matmul_mx(
                 out=z_ps[g][:, r, :],
@@ -137,7 +162,7 @@ def tile_rows_gmlp_tanh_kernel(tc, x, w1, hs, w2, out):
             )
 
         def second_layer(u, dst):
-            g = u % G
+            g = ORDER[u][1]
             nc.tensor.matmul_mx(
                 out=dst,
                 lhsT=w2_codes[:, g, :].bitcast(FP8X4),
@@ -148,51 +173,66 @@ def tile_rows_gmlp_tanh_kernel(tc, x, w1, hs, w2, out):
                 stop=True,
             )
 
-        on_vector, on_scalar = nc.vector.tensor_copy, nc.scalar.copy
-        scalar_jobs = {"lay_x": lay_x, "lay_w2": lay_w2}
-        vector_jobs = {
-            "lay_x": lambda c: lay_x(on_vector, c),
-            "quant_x": quant_x,
-            "quant_h": quant_h,
-            "quant_w2": quant_w2,
-        }
+        copies = {"V": nc.vector.tensor_copy, "S": nc.scalar.copy}
 
-        dst, src = dealt(0, W1_SPLIT)
-        nc.vector.tensor_copy(out=dst, in_=src)
-        dst, src = dealt(W1_SPLIT, P)
-        nc.scalar.activation(out=dst, in_=src, func=ACT.Copy)
-        lay_x(on_vector, 0, 0, X0_SPLIT)
-        lay_x(on_scalar, 0, X0_SPLIT, COLS)
-        quant_w1(0)
-        quant_x(0)
-        for r in range(1, PACK):
-            quant_w1(r)
-        lay_x(on_scalar, 1)
-        lay_w2(on_vector, 0)
-        lay_w2(on_vector, 1)
-        quant_x(1)
-        quant_w2(0, 2)
-
-        for u in range(UNITS):
-            g = u % G
-            for r in range(PACK):
-                first_layer(u, r)
-            nc.scalar.activation(out=tanh_z[:, u, :, :], in_=z_ps[g][:].rearrange("s r n -> s n r"), func=ACT.Tanh)
-            if u in SCALAR_EXTRAS:
-                job, index = SCALAR_EXTRAS[u]
-                scalar_jobs[job](on_scalar, index)
-            scale = hs_sb[:, g, 0:PACK].unsqueeze(1).broadcast_to([P, COLS, PACK])
-            nc.vector.tensor_tensor(out=h_bf[:, u, :, :], in0=tanh_z[:, u, :, :], in1=scale, op=ALU.mult)
-            for job in VECTOR_EXTRAS.get(u, []):
-                vector_jobs[job[0]](*job[1:])
-
-        for i, (c0, chunks, g0, groups, bank) in enumerate(PIECES):
+        def piece_matmuls(i):
+            c0, chunks, g0, groups, bank = PIECES[i]
             for c in range(chunks):
                 for g in range(groups):
-                    second_layer(G * (c0 + c) + g0 + g, y_ps[bank][:, g * chunks + c, :])
-            nc.scalar.copy(
+                    second_layer(ORDER.index((c0 + c, g0 + g)), y_ps[bank][:, g * chunks + c, :])
+
+        def piece_out(engine, i):
+            c0, chunks, g0, groups, bank = PIECES[i]
+            copies[engine](
                 out=y_sb[i][:].rearrange("m g n -> m (g n)"),
                 in_=y_ps[bank][:, 0 : groups * chunks, :].rearrange("m a n -> m (a n)"),
             )
             out_piece = out[g0 : g0 + groups, :, c0 * COLS : (c0 + chunks) * COLS]
             nc.sync.dma_start(out=out_piece.rearrange("g m n -> m g n"), in_=y_sb[i][:])
+
+        def mult(u, count=1):
+            g = ORDER[u][1]
+            scale = hs_sb[:, g : g + count, 0:PACK].unsqueeze(2).broadcast_to([P, count, COLS, PACK])
+            nc.vector.tensor_tensor(out=h_bf[:, u : u + count, :, :], in0=tanh_z[:, u : u + count, :, :], in1=scale, op=ALU.mult)
+
+        def mult_half(u, half):
+            cols = slice(half * COLS // 2, (half + 1) * COLS // 2)
+            scale = hs_sb[:, ORDER[u][1], 0:PACK].unsqueeze(1).broadcast_to([P, COLS // 2, PACK])
+            nc.vector.tensor_tensor(out=h_bf[:, u, cols, :], in0=tanh_z[:, u, cols, :], in1=scale, op=ALU.mult)
+
+        def unit_matmuls(u):
+            for r in range(PACK):
+                first_layer(u, r)
+
+        jobs = {
+            "lay_x": lambda e, *a: lay_x(copies[e], *a),
+            "lay_w2": lambda e, *a: lay_w2(copies[e], *a),
+            "quant_x": quant_x,
+            "quant_w1": quant_w1,
+            "quant_w2": quant_w2,
+            "quant_h": quant_h,
+            "mm2": piece_matmuls,
+            "out": piece_out,
+            "mm1": unit_matmuls,
+            "mult": mult,
+            "mult_half": mult_half,
+        }
+
+        def run(steps):
+            for step in steps:
+                jobs[step[0]](*step[1:])
+
+        dst, src = dealt(0, W1_SPLIT)
+        nc.vector.tensor_copy(out=dst, in_=src)
+        dst, src = dealt(W1_SPLIT, P)
+        nc.scalar.activation(out=dst, in_=src, func=ACT.Copy)
+        run(HEAD)
+        for u in range(UNITS):
+            g = ORDER[u][1]
+            parts = 2 if u in HALVED else 1
+            for part in range(parts):
+                cols = slice(part * COLS // parts, (part + 1) * COLS // parts)
+                nc.scalar.activation(out=tanh_z[:, u, cols, :], in_=z_ps[g][:, :, cols].rearrange("s r n -> s n r"), func=ACT.Tanh)
+            run(AFTER_TANH.get(u, []))
+            run(AFTER_MULT.get(u, [("mult", u)]))
+        run(TAIL)

@@ -54,7 +54,7 @@ AFTER_MULT = {
     14: [("mult",14,), ("quant_h",12,2,)],
     15: [("mult_half",15,0,), ("mult_half",15,1,), ("quant_h",14,1,), ("quant_h",15,1,)],
 }
-TAIL = [("mm2",2,), ("out","S",2,), ("mm2",3,), ("out","S",3,), ("mm2",4,), ("out","S",4,), ("mm2",5,), ("out","S",5,), ("mm2",6,), ("out","V",6,)]
+TAIL = [("mm2",2,), ("out","S",2,), ("mm2",3,), ("out","S",3,), ("mm2",4,), ("out","S",4,), ("mm2",5,), ("out","S",5,), ("mm2",6,), ("out","S",6,)]
 PIECES = [(0,2,0,2,0,), (0,2,2,2,1,), (2,1,0,2,2,), (2,1,2,2,3,), (3,1,0,2,0,), (3,1,2,1,1,), (3,1,3,1,2,)]
 
 

@@ -25,9 +25,9 @@ ALIGN = 64
 W1_SPLIT = 80
 X0_SPLIT = 96
 ORDER = [(0,0), (0,1), (0,2), (0,3), (1,0), (1,1), (1,2), (1,3), (2,0), (2,1), (2,2), (2,3), (3,0), (3,1), (3,2), (3,3)]
-HALVED = [15]
+HALVED = []
 LOADS = [("w1",), ("x",0,1,), ("w2",0,1,), ("w2",1,1,), ("x",1,1,), ("hs",0,4,), ("x",2,2,), ("w2",2,2,)]
-HEAD = [("lay_x","V",0,0,96,), ("lay_x","S",0,96,128,), ("quant_w1",0,), ("quant_x",0,), ("quant_w1",1,), ("quant_w1",2,), ("quant_w1",3,), ("lay_w2","S",0,), ("lay_w2","S",1,), ("quant_w2",0,1,), ("lay_x","V",1,), ("quant_w2",1,1,), ("quant_x",1,), ("mm1",0,), ("mm1",1,), ("mm1",2,), ("mm1",3,)]
+HEAD = [("lay_x","V",0,0,96,), ("lay_x","S",0,96,128,), ("quant_w1",0,), ("quant_x",0,), ("quant_w1",1,), ("quant_w1",2,), ("quant_w1",3,), ("lay_w2","S",0,), ("lay_w2","S",1,), ("quant_w2",0,1,), ("lay_x","V",1,), ("quant_w2",1,1,), ("quant_x",1,), ("mm1",0,2,), ("mm1",2,2,)]
 AFTER_TANH = {
     0: [("mm1",4,)],
     1: [("mm1",5,)],
@@ -36,26 +36,30 @@ AFTER_TANH = {
     4: [("mm1",8,)],
     5: [("mm1",9,)],
     6: [("mm1",10,)],
-    7: [("mm1",11,)],
-    8: [("mm1",12,), ("lay_w2","S",2,)],
-    9: [("mm1",13,), ("mm2",0,), ("lay_w2","S",3,)],
-    10: [("mm1",14,), ("mm2",1,)],
-    11: [("mm1",15,)],
-    12: [("out","S",0,)],
-    14: [("out","S",1,)],
+    7: [("mm1",11,), ("lay_w2","S",2,)],
+    8: [("mm1",12,)],
+    9: [("mm1",13,)],
+    10: [("mm1",14,)],
+    11: [("mm1",15,), ("mm2",0,), ("lay_w2","S",3,)],
+    14: [],
 }
 AFTER_MULT = {
     2: [("mult",2,), ("lay_x","V",2,)],
-    3: [("mult",3,), ("quant_x",2,), ("quant_x",3,)],
+    3: [("mult",3,), ("quant_x23",)],
     5: [("mult",5,), ("quant_h",0,4,)],
+    6: [],
+    7: [("mult",6,2,)],
     8: [("mult",8,), ("quant_h",4,4,)],
-    9: [("mult",9,), ("quant_w2",2,2,)],
-    12: [("mult",12,), ("quant_h",8,4,)],
+    9: [],
+    10: [("mult",9,2,)],
+    11: [("mult",11,), ("quant_w2",2,2,), ("quant_h",8,4,)],
+    12: [],
+    13: [("mult",12,2,)],
     14: [("mult",14,), ("quant_h",12,2,)],
-    15: [("mult_half",15,0,), ("mult_half",15,1,), ("quant_h",14,1,), ("quant_h",15,1,)],
+    15: [("mult",15,), ("quant_h",14,1,), ("quant_h",15,1,)],
 }
-TAIL = [("mm2",2,), ("out","S",2,), ("mm2",3,), ("out","S",3,), ("mm2",4,), ("out","S",4,), ("mm2",5,), ("out","S",5,), ("mm2",6,), ("out","S",6,)]
-PIECES = [(0,2,0,2,0,), (0,2,2,2,1,), (2,1,0,2,2,), (2,1,2,2,3,), (3,1,0,2,0,), (3,1,2,1,1,), (3,1,3,1,2,)]
+TAIL = [("out","S",0,), ("mm2",1,), ("out","S",1,), ("mm2",2,), ("out","S",2,), ("mm2",3,), ("out","S",3,), ("mm2",4,), ("out","S",4,), ("mm2",5,), ("out","S",5,)]
+PIECES = [(0,2,0,2,0,), (0,2,2,2,1,), (2,1,0,4,2,), (3,1,0,2,3,), (3,1,2,1,0,), (3,1,3,1,1,)]
 
 
 def tile_rows_gmlp_tanh_kernel(tc, x, w1, hs, w2, out):
@@ -75,9 +79,15 @@ def tile_rows_gmlp_tanh_kernel(tc, x, w1, hs, w2, out):
         w2_raw = sbuf("w2_raw", [G, PACK * M], F32)
         hs_sb = sbuf("hs_sb", [G, HS_PITCH], F32)
         x_raw = {}
-        x_bf = [sbuf("x_bf%d" % c, [COLS, PACK], BF16) for c in range(CHUNKS)]
-        x_codes = [sbuf("x_codes%d" % c, [COLS], U32) for c in range(CHUNKS)]
-        x_scales = [sbuf("x_scales%d" % c, [COLS], U8) for c in range(CHUNKS)]
+        x_bf = [sbuf("x_bf%d" % c, [COLS, PACK], BF16) for c in range(2)]
+        x_codes = [sbuf("x_codes%d" % c, [COLS], U32) for c in range(2)]
+        x_scales = [sbuf("x_scales%d" % c, [COLS], U8) for c in range(2)]
+        late_bf = sbuf("x_bf23", [2, COLS, PACK], BF16)
+        late_codes = sbuf("x_codes23", [2, COLS], U32)
+        late_scales = sbuf("x_scales23", [2, COLS], U8)
+        x_bf = x_bf + [late_bf[:, c, :, :] for c in range(2)]
+        x_codes = x_codes + [late_codes[:, c, :] for c in range(2)]
+        x_scales = x_scales + [late_scales[:, c, :] for c in range(2)]
         w1_bf = sbuf("w1_bf", [PACK, P, PACK], BF16)
         w1_codes = sbuf("w1_codes", [PACK, P], U32)
         w1_scales = sbuf("w1_scales", [PACK, P], U8)
@@ -200,9 +210,13 @@ def tile_rows_gmlp_tanh_kernel(tc, x, w1, hs, w2, out):
             scale = hs_sb[:, ORDER[u][1], 0:PACK].unsqueeze(1).broadcast_to([P, COLS // 2, PACK])
             nc.vector.tensor_tensor(out=h_bf[:, u, cols, :], in0=tanh_z[:, u, cols, :], in1=scale, op=ALU.mult)
 
-        def unit_matmuls(u):
+        def quant_x23():
+            quant(late_codes[:].rearrange("p c n -> p (c n)"), late_scales[:].rearrange("p c n -> p (c n)"), late_bf[:].rearrange("p c n j -> p (c n j)"))
+
+        def unit_matmuls(u, count=1):
             for r in range(PACK):
-                first_layer(u, r)
+                for unit in range(u, u + count):
+                    first_layer(unit, r)
 
         jobs = {
             "lay_x": lambda e, *a: lay_x(copies[e], *a),
@@ -215,6 +229,7 @@ def tile_rows_gmlp_tanh_kernel(tc, x, w1, hs, w2, out):
             "out": piece_out,
             "mm1": unit_matmuls,
             "mult": mult,
+            "quant_x23": quant_x23,
             "mult_half": mult_half,
         }
 

@@ -44,6 +44,7 @@ AFTER_TANH = {
     14: [],
 }
 AFTER_MULT = {
+    0: [("mult_first",)],
     2: [("mult",2,), ("lay_x","V",2,)],
     3: [("mult",3,), ("quant_x23",)],
     5: [("mult",5,), ("quant_h",0,4,)],
@@ -59,7 +60,7 @@ AFTER_MULT = {
     15: [("mult",15,), ("quant_h",14,1,), ("quant_h",15,1,)],
 }
 TAIL = [("out","S",0,), ("mm2",1,), ("out","S",1,), ("mm2",2,), ("out","S",2,), ("mm2",3,), ("out","S",3,), ("mm2",4,), ("out","S",4,), ("mm2",5,), ("out","S",5,)]
-PIECES = [(0,2,0,2,0,), (0,2,2,2,1,), (2,1,0,4,2,), (3,1,0,2,3,), (3,1,2,1,0,), (3,1,3,1,1,)]
+PIECES = [(0,2,0,2,0,), (0,2,2,2,1,), (2,1,0,4,2,), (3,1,0,2,0,), (3,1,2,1,1,), (3,1,3,1,2,)]
 
 
 def tile_rows_gmlp_tanh_kernel(tc, x, w1, hs, w2, out):
@@ -100,7 +101,8 @@ def tile_rows_gmlp_tanh_kernel(tc, x, w1, hs, w2, out):
         h_scales = sbuf("h_scales", [UNITS, COLS], U8)
         y_sb = [sbuf("y_sb%d" % i, [piece[3], piece[1] * COLS], F32) for i, piece in enumerate(PIECES)]
         z_ps = [ps.tile([P, PACK, COLS], F32, name="z_ps%d" % g) for g in range(G)]
-        y_ps = [ps.tile([P, PACK, COLS], F32, name="y_ps%d" % b) for b in range(4)]
+        z_side = ps.tile([P, PACK, COLS], F32, name="z_side")
+        y_ps = [ps.tile([P, PACK, COLS], F32, name="y_ps%d" % b) for b in range(3)]
 
         for load in LOADS:
             if load[0] == "w1":
@@ -162,7 +164,7 @@ def tile_rows_gmlp_tanh_kernel(tc, x, w1, hs, w2, out):
             c, g = ORDER[u]
             rows = slice(ROWS * g, ROWS * (g + 1))
             nc.tensor.matmul_mx(
-                out=z_ps[g][:, r, :],
+                out=(z_side if u == 0 and r >= 2 else z_ps[g])[:, r, :],
                 lhsT=w1_codes[rows, r, :].bitcast(FP8X4),
                 lhsT_scale=w1_scales[rows, r, :],
                 rhs=x_codes[c][rows, :].bitcast(FP8X4),
@@ -213,6 +215,11 @@ def tile_rows_gmlp_tanh_kernel(tc, x, w1, hs, w2, out):
         def quant_x23():
             quant(late_codes[:].rearrange("p c n -> p (c n)"), late_scales[:].rearrange("p c n -> p (c n)"), late_bf[:].rearrange("p c n j -> p (c n j)"))
 
+        def mult_first():
+            halves = tanh_z[:, 0, :, :].rearrange("s n r -> s (n r)").rearrange("s (h n e) -> s n h e", h=2, e=2)
+            scale = hs_sb[:, ORDER[0][1], 0:PACK].rearrange("s (h e) -> s h e", h=2).unsqueeze(1).broadcast_to([P, COLS, 2, 2])
+            nc.vector.tensor_tensor(out=h_bf[:, 0, :, :].rearrange("s n (h e) -> s n h e", h=2), in0=halves, in1=scale, op=ALU.mult)
+
         def unit_matmuls(u, count=1):
             for r in range(PACK):
                 for unit in range(u, u + count):
@@ -229,6 +236,7 @@ def tile_rows_gmlp_tanh_kernel(tc, x, w1, hs, w2, out):
             "out": piece_out,
             "mm1": unit_matmuls,
             "mult": mult,
+            "mult_first": mult_first,
             "quant_x23": quant_x23,
             "mult_half": mult_half,
         }
@@ -244,10 +252,12 @@ def tile_rows_gmlp_tanh_kernel(tc, x, w1, hs, w2, out):
         run(HEAD)
         for u in range(UNITS):
             g = ORDER[u][1]
-            parts = 2 if u in HALVED else 1
-            for part in range(parts):
-                cols = slice(part * COLS // parts, (part + 1) * COLS // parts)
-                nc.scalar.activation(out=tanh_z[:, u, cols, :], in_=z_ps[g][:, :, cols].rearrange("s r n -> s n r"), func=ACT.Tanh)
+            if u == 0:
+                halves = tanh_z[:, 0, :, :].rearrange("s n r -> s (n r)").rearrange("s (h n e) -> s h n e", h=2, e=2)
+                for half, bank in enumerate((z_ps[g], z_side)):
+                    nc.scalar.activation(out=halves[:, half, :, :], in_=bank[:, 2 * half : 2 * half + 2, :].rearrange("s e n -> s n e"), func=ACT.Tanh)
+            else:
+                nc.scalar.activation(out=tanh_z[:, u, :, :], in_=z_ps[g][:].rearrange("s r n -> s n r"), func=ACT.Tanh)
             run(AFTER_TANH.get(u, []))
             run(AFTER_MULT.get(u, [("mult", u)]))
         run(TAIL)

@@ -27,7 +27,7 @@ X0_SPLIT = 96
 ORDER = [(0,0), (0,1), (0,2), (0,3), (1,0), (1,1), (1,2), (1,3), (2,0), (2,1), (2,2), (2,3), (3,0), (3,1), (3,2), (3,3)]
 HALVED = []
 LOADS = [("w1",), ("x",0,1,), ("w2",0,1,), ("w2",1,1,), ("x",1,1,), ("hs",0,4,), ("x",2,2,), ("w2",2,2,)]
-HEAD = [("lay_x","V",0,0,96,), ("lay_x","S",0,96,128,), ("quant_w1",0,), ("quant_x",0,), ("quant_w1",1,), ("quant_w1",2,), ("quant_w1",3,), ("lay_w2","S",0,), ("lay_w2","S",1,), ("quant_w2",0,1,), ("lay_x","V",1,), ("quant_w2",1,1,), ("quant_x",1,), ("mm1",0,2,), ("mm1",2,2,)]
+HEAD = [("lay_x","V",0,0,96,), ("lay_x","S",0,96,128,), ("quant_w1",0,), ("quant_x",0,), ("quant_w1",1,), ("quant_w1",2,), ("quant_w1",3,), ("lay_w2","S",0,), ("lay_w2","V",1,), ("quant_w2",0,1,), ("lay_x","V",1,), ("quant_w2",1,1,), ("quant_x",1,), ("mm1",0,2,), ("mm1",2,2,)]
 AFTER_TANH = {
     0: [("mm1",4,)],
     1: [("mm1",5,)],

@@ -26,28 +26,27 @@ W1_SPLIT = 80
 X0_SPLIT = 96
 ORDER = [(0,0), (0,1), (0,2), (0,3), (1,0), (1,1), (1,2), (1,3), (2,0), (2,1), (2,2), (2,3), (3,0), (3,1), (3,2), (3,3)]
 HALVED = []
-LOADS = [("w1",), ("x",0,1,), ("w2",0,1,), ("w2",1,1,), ("x",1,1,), ("hs",0,4,), ("x",2,2,), ("w2",2,2,)]
-HEAD = [("lay_x","V",0,0,96,), ("lay_x","S",0,96,128,), ("quant_w1",0,), ("quant_x",0,), ("quant_w1",1,), ("quant_w1",2,), ("quant_w1",3,), ("lay_w2","S",0,), ("lay_w2","V",1,), ("quant_w2",0,1,), ("lay_x","V",1,), ("quant_w2",1,1,), ("quant_x",1,), ("mm1",0,2,), ("mm1",2,2,)]
+LOADS = [("w1",), ("x",0,1,), ("x",1,1,), ("w2",0,1,), ("w2",1,1,), ("hs",0,4,), ("x",2,2,), ("w2",2,2,)]
+HEAD = [("lay_x","V",0,0,96,), ("lay_x","S",0,96,128,), ("quant_w1",0,), ("quant_x",0,), ("quant_w1",1,), ("quant_w1",2,), ("quant_w1",3,), ("lay_x","S",1,), ("lay_w2","V",0,), ("quant_x",1,), ("lay_w2","V",1,), ("quant_w2",0,2,), ("mm1",0,2,), ("mm1",2,2,)]
 AFTER_TANH = {
     0: [("mm1",4,)],
     1: [("mm1",5,)],
     2: [("mm1",6,)],
-    3: [("mm1",7,), ("lay_x","S",3,)],
-    4: [("mm1",8,)],
+    3: [("mm1",7,)],
+    4: [("mm1",8,), ("lay_x","S",3,)],
     5: [("mm1",9,)],
     6: [("mm1",10,)],
     7: [("mm1",11,), ("lay_w2","S",2,)],
     8: [("mm1",12,)],
     9: [("mm1",13,)],
     10: [("mm1",14,)],
-    11: [("mm1",15,), ("mm2",0,), ("lay_w2","S",3,)],
-    14: [],
+    11: [("mm1",15,), ("lay_w2","S",3,)],
 }
 AFTER_MULT = {
     0: [("mult_first",)],
-    2: [("mult",2,), ("lay_x","V",2,)],
-    3: [("mult",3,), ("quant_x23",)],
-    5: [("mult",5,), ("quant_h",0,4,)],
+    2: [("mult",2,), ("lay_x","V",2,0,128,)],
+    3: [("mult",3,), ("quant_x",2,)],
+    5: [("mult",5,), ("quant_h",0,4,), ("quant_x",3,)],
     6: [],
     7: [("mult",6,2,)],
     8: [("mult",8,), ("quant_h",4,4,)],
@@ -59,7 +58,7 @@ AFTER_MULT = {
     14: [("mult",14,), ("quant_h",12,2,)],
     15: [("mult",15,), ("quant_h",14,1,), ("quant_h",15,1,)],
 }
-TAIL = [("out","S",0,), ("mm2",1,), ("out","S",1,), ("mm2",2,), ("out","S",2,), ("mm2",3,), ("out","S",3,), ("mm2",4,), ("out","S",4,), ("mm2",5,), ("out","S",5,)]
+TAIL = [("mm2",0,), ("out","S",0,), ("mm2",1,), ("out","S",1,), ("mm2",2,), ("out","S",2,), ("mm2",3,), ("out","S",3,), ("mm2",4,), ("out","S",4,), ("mm2",5,), ("out","S",5,)]
 PIECES = [(0,2,0,2,0,), (0,2,2,2,1,), (2,1,0,4,2,), (3,1,0,2,0,), (3,1,2,1,1,), (3,1,3,1,2,)]
 
 
@@ -80,15 +79,9 @@ def tile_rows_gmlp_tanh_kernel(tc, x, w1, hs, w2, out):
         w2_raw = sbuf("w2_raw", [G, PACK * M], F32)
         hs_sb = sbuf("hs_sb", [G, HS_PITCH], F32)
         x_raw = {}
-        x_bf = [sbuf("x_bf%d" % c, [COLS, PACK], BF16) for c in range(2)]
-        x_codes = [sbuf("x_codes%d" % c, [COLS], U32) for c in range(2)]
-        x_scales = [sbuf("x_scales%d" % c, [COLS], U8) for c in range(2)]
-        late_bf = sbuf("x_bf23", [2, COLS, PACK], BF16)
-        late_codes = sbuf("x_codes23", [2, COLS], U32)
-        late_scales = sbuf("x_scales23", [2, COLS], U8)
-        x_bf = x_bf + [late_bf[:, c, :, :] for c in range(2)]
-        x_codes = x_codes + [late_codes[:, c, :] for c in range(2)]
-        x_scales = x_scales + [late_scales[:, c, :] for c in range(2)]
+        x_bf = [sbuf("x_bf%d" % c, [COLS, PACK], BF16) for c in range(CHUNKS)]
+        x_codes = [sbuf("x_codes%d" % c, [COLS], U32) for c in range(CHUNKS)]
+        x_scales = [sbuf("x_scales%d" % c, [COLS], U8) for c in range(CHUNKS)]
         w1_bf = sbuf("w1_bf", [PACK, P, PACK], BF16)
         w1_codes = sbuf("w1_codes", [PACK, P], U32)
         w1_scales = sbuf("w1_scales", [PACK, P], U8)
@@ -212,9 +205,6 @@ def tile_rows_gmlp_tanh_kernel(tc, x, w1, hs, w2, out):
             scale = hs_sb[:, ORDER[u][1], 0:PACK].unsqueeze(1).broadcast_to([P, COLS // 2, PACK])
             nc.vector.tensor_tensor(out=h_bf[:, u, cols, :], in0=tanh_z[:, u, cols, :], in1=scale, op=ALU.mult)
 
-        def quant_x23():
-            quant(late_codes[:].rearrange("p c n -> p (c n)"), late_scales[:].rearrange("p c n -> p (c n)"), late_bf[:].rearrange("p c n j -> p (c n j)"))
-
         def mult_first():
             halves = tanh_z[:, 0, :, :].rearrange("s n r -> s (n r)").rearrange("s (h n e) -> s n h e", h=2, e=2)
             scale = hs_sb[:, ORDER[0][1], 0:PACK].rearrange("s (h e) -> s h e", h=2).unsqueeze(1).broadcast_to([P, COLS, 2, 2])
@@ -237,7 +227,6 @@ def tile_rows_gmlp_tanh_kernel(tc, x, w1, hs, w2, out):
             "mm1": unit_matmuls,
             "mult": mult,
             "mult_first": mult_first,
-            "quant_x23": quant_x23,
             "mult_half": mult_half,
         }
 

@@ -33,22 +33,25 @@ AFTER_TANH = {
     1: [("mm1",5,)],
     2: [("mm1",6,)],
     3: [("mm1",7,)],
-    4: [("mm1",8,), ("lay_x","S",3,)],
+    4: [("lay_x","S",2,0,64,)],
     5: [("mm1",9,)],
     6: [("mm1",10,)],
-    7: [("mm1",11,), ("lay_w2","S",2,)],
+    7: [("mm1",11,), ("lay_x","S",3,)],
     8: [("mm1",12,)],
     9: [("mm1",13,)],
-    10: [("mm1",14,)],
-    11: [("mm1",15,), ("lay_w2","S",3,)],
+    10: [("mm1",14,), ("lay_w2","S",2,)],
+    11: [("mm1",15,), ("mm2",0,), ("lay_w2","S",3,)],
+    14: [("out","S",0,)],
 }
 AFTER_MULT = {
     0: [("mult_first",)],
-    2: [("mult",2,), ("lay_x","V",2,0,128,)],
-    3: [("mult",3,), ("quant_x",2,)],
-    5: [("mult",5,), ("quant_h",0,4,), ("quant_x",3,)],
+    1: [("mult",1,)],
+    2: [("mult",2,), ("lay_x","V",2,64,128,)],
+    3: [("mult",3,)],
+    4: [("quant_x",2,), ("mm1",8,), ("mult",4,)],
+    5: [("mult",5,), ("quant_h",0,4,)],
     6: [],
-    7: [("mult",6,2,)],
+    7: [("mult",6,2,), ("quant_x",3,)],
     8: [("mult",8,), ("quant_h",4,4,)],
     9: [],
     10: [("mult",9,2,)],
@@ -58,7 +61,7 @@ AFTER_MULT = {
     14: [("mult",14,), ("quant_h",12,2,)],
     15: [("mult",15,), ("quant_h",14,1,), ("quant_h",15,1,)],
 }
-TAIL = [("mm2",0,), ("out","S",0,), ("mm2",1,), ("out","S",1,), ("mm2",2,), ("out","S",2,), ("mm2",3,), ("out","S",3,), ("mm2",4,), ("out","S",4,), ("mm2",5,), ("out","S",5,)]
+TAIL = [("mm2",1,), ("out","S",1,), ("mm2",2,), ("out","S",2,), ("mm2",3,), ("out","S",3,), ("mm2",4,), ("out","S",4,), ("mm2",5,), ("out","S",5,)]
 PIECES = [(0,2,0,2,0,), (0,2,2,2,1,), (2,1,0,4,2,), (3,1,0,2,0,), (3,1,2,1,1,), (3,1,3,1,2,)]
 
 

@@ -22,47 +22,7 @@ UNITS = G * CHUNKS
 HS_PITCH = 8
 ALIGN = 64
 
-W1_SPLIT = 80
-X0_SPLIT = 96
-ORDER = [(0,0), (0,1), (0,2), (0,3), (1,0), (1,1), (1,2), (1,3), (2,0), (2,1), (2,2), (2,3), (3,0), (3,1), (3,2), (3,3)]
-HALVED = []
-LOADS = [("w1",), ("x",0,1,), ("x",1,1,), ("w2",0,1,), ("w2",1,1,), ("hs",0,4,), ("x",2,2,), ("w2",2,2,)]
-HEAD = [("lay_x","V",0,0,96,), ("lay_x","S",0,96,128,), ("quant_w1",0,), ("quant_x",0,), ("quant_w1",1,), ("quant_w1",2,), ("quant_w1",3,), ("lay_x","S",1,), ("lay_w2","V",0,), ("quant_x",1,), ("lay_w2","V",1,), ("quant_w2",0,2,), ("mm1",0,2,), ("mm1",2,2,)]
-AFTER_TANH = {
-    0: [("mm1",4,)],
-    1: [("mm1",5,)],
-    2: [("mm1",6,)],
-    3: [("mm1",7,)],
-    4: [("lay_x","S",2,0,64,)],
-    5: [("mm1",9,)],
-    6: [("mm1",10,)],
-    7: [("mm1",11,), ("lay_x","S",3,)],
-    8: [("mm1",12,)],
-    9: [("mm1",13,)],
-    10: [("mm1",14,), ("lay_w2","S",2,)],
-    11: [("mm1",15,), ("mm2",0,), ("lay_w2","S",3,)],
-    14: [("out","S",0,)],
-}
-AFTER_MULT = {
-    0: [("mult_first",)],
-    1: [("mult",1,)],
-    2: [("mult",2,), ("lay_x","V",2,64,128,)],
-    3: [("mult",3,)],
-    4: [("quant_x",2,), ("mm1",8,), ("mult",4,)],
-    5: [("mult",5,), ("quant_h",0,4,)],
-    6: [],
-    7: [("mult",6,2,), ("quant_x",3,)],
-    8: [("mult",8,), ("quant_h",4,4,)],
-    9: [],
-    10: [("mult",9,2,)],
-    11: [("mult",11,), ("quant_w2",2,2,), ("quant_h",8,4,)],
-    12: [],
-    13: [("mult",12,2,)],
-    14: [("mult",14,), ("quant_h",12,2,)],
-    15: [("mult",15,), ("quant_h",14,1,), ("quant_h",15,1,)],
-}
-TAIL = [("mm2",1,), ("out","S",1,), ("mm2",2,), ("out","S",2,), ("mm2",3,), ("out","S",3,), ("mm2",4,), ("out","S",4,), ("mm2",5,), ("out","S",5,)]
-PIECES = [(0,2,0,2,0,), (0,2,2,2,1,), (2,1,0,4,2,), (3,1,0,2,0,), (3,1,2,1,1,), (3,1,3,1,2,)]
+DMA_ALIGN = 256
 
 
 def tile_rows_gmlp_tanh_kernel(tc, x, w1, hs, w2, out):
@@ -72,15 +32,16 @@ def tile_rows_gmlp_tanh_kernel(tc, x, w1, hs, w2, out):
         ps = ctx.enter_context(tc.psum_pool(name="ps", bufs=1))
         ctx.enter_context(tc.manual_schedule())
 
-        def sbuf(name, shape, dtype):
-            return sb.tile([P] + shape, dtype, name=name, align_bytes=ALIGN)
+        def sbuf(name, shape, dtype, align=ALIGN):
+            return sb.tile([P] + shape, dtype, name=name, align_bytes=align)
 
         x_hbm = x.flatten_outer_dims().rearrange("(p j) n -> p j n", j=PACK)
         w1_hbm = w1.flatten_outer_dims().rearrange("(p j) k -> p j k", j=PACK)
         w2_hbm = w2.rearrange("g (s r) m -> s g (r m)", r=PACK)
-        w1_raw = sbuf("w1_raw", [PACK, K], F32)
-        w2_raw = sbuf("w2_raw", [G, PACK * M], F32)
-        hs_sb = sbuf("hs_sb", [G, HS_PITCH], F32)
+        hs_hbm = hs.rearrange("g (s r) o -> s g (r o)", r=PACK)
+        w1_raw = sbuf("w1_raw", [PACK, K], F32, DMA_ALIGN)
+        w2_raw = sbuf("w2_raw", [G, PACK * M], F32, DMA_ALIGN)
+        hs_sb = sbuf("hs_sb", [G, HS_PITCH], F32, DMA_ALIGN)
         x_raw = {}
         x_bf = [sbuf("x_bf%d" % c, [COLS, PACK], BF16) for c in range(CHUNKS)]
         x_codes = [sbuf("x_codes%d" % c, [COLS], U32) for c in range(CHUNKS)]
@@ -95,26 +56,26 @@ def tile_rows_gmlp_tanh_kernel(tc, x, w1, hs, w2, out):
         h_bf = sbuf("h_bf", [UNITS, COLS, PACK], BF16)
         h_codes = sbuf("h_codes", [UNITS, COLS], U32)
         h_scales = sbuf("h_scales", [UNITS, COLS], U8)
-        y_sb = [sbuf("y_sb%d" % i, [piece[3], piece[1] * COLS], F32) for i, piece in enumerate(PIECES)]
         z_ps = [ps.tile([P, PACK, COLS], F32, name="z_ps%d" % g) for g in range(G)]
         z_side = ps.tile([P, PACK, COLS], F32, name="z_side")
         y_ps = [ps.tile([P, PACK, COLS], F32, name="y_ps%d" % b) for b in range(3)]
 
-        for load in LOADS:
-            if load[0] == "w1":
-                nc.sync.dma_start(out=w1_raw[:], in_=w1_hbm)
-            elif load[0] == "x":
-                first, count = load[1:]
-                raw = sbuf("x_raw%d" % first, [PACK, count * COLS], F32)
-                nc.sync.dma_start(out=raw[:], in_=x_hbm[:, :, first * COLS : (first + count) * COLS])
-                for c in range(count):
-                    x_raw[first + c] = raw[:, :, c * COLS : (c + 1) * COLS]
-            elif load[0] == "w2":
-                groups = slice(load[1], load[1] + load[2])
-                nc.sync.dma_start(out=w2_raw[:, groups, :], in_=w2_hbm[:, groups, :])
-            else:
-                groups = slice(load[1], load[1] + load[2])
-                nc.sync.dma_start(out=hs_sb[:, groups, 0:PACK], in_=hs.rearrange("g (s r) o -> s g (r o)", r=PACK)[:, groups, :])
+        def load_w1():
+            nc.sync.dma_start(out=w1_raw[:], in_=w1_hbm)
+
+        def load_x(first, count):
+            raw = sbuf("x_raw%d" % first, [PACK, count * COLS], F32, DMA_ALIGN)
+            nc.sync.dma_start(out=raw[:], in_=x_hbm[:, :, first * COLS : (first + count) * COLS])
+            for c in range(count):
+                x_raw[first + c] = raw[:, :, c * COLS : (c + 1) * COLS]
+
+        def load_w2(first, count):
+            groups = slice(first, first + count)
+            nc.sync.dma_start(out=w2_raw[:, groups, :], in_=w2_hbm[:, groups, :])
+
+        def load_hs(first=0, count=G):
+            groups = slice(first, first + count)
+            nc.sync.dma_start(out=hs_sb[:, groups, 0:PACK], in_=hs_hbm[:, groups, :])
 
         def lay(copy, dst, src):
             copy(out=dst.rearrange("p (c i) j -> p c j i", i=4), in_=src.rearrange("p j (c i) -> p c j i", i=4))
@@ -125,10 +86,10 @@ def tile_rows_gmlp_tanh_kernel(tc, x, w1, hs, w2, out):
         def lay_w2(copy, g, m0=0, m1=M):
             lay(copy, w2_bf[:, g, m0:m1, :], w2_raw[:, g, :].rearrange("s (r m) -> s r m", r=PACK)[:, :, m0:m1])
 
-        def dealt(s0, s1):
-            dst = w1_bf[:, :, s0:s1, :].rearrange("p r s j -> p s j r")
-            src = w1_raw[:, :, PACK * s0 : PACK * s1].rearrange("p j (s r) -> p s j r", r=PACK)
-            return dst, src
+        def deal_w1(copy, r0, r1, s0=0, s1=P):
+            dst = w1_bf[:, r0:r1, s0:s1, :].rearrange("p r s j -> p s j r")
+            src = w1_raw[:].rearrange("p j (s r) -> p s j r", r=PACK)[:, s0:s1, :, r0:r1]
+            copy(out=dst, in_=src)
 
         def quant(codes, scales, values):
             nc.vector.quantize_mx(out=codes.bitcast(FP8X4), scales=scales, in_=values)
@@ -136,120 +97,188 @@ def tile_rows_gmlp_tanh_kernel(tc, x, w1, hs, w2, out):
         def quant_x(c):
             quant(x_codes[c][:], x_scales[c][:], x_bf[c][:].rearrange("p n j -> p (n j)"))
 
-        def quant_w1(r, count=1):
-            rs = slice(r, r + count)
-            quant(w1_codes[:, rs, :].rearrange("p r s -> p (r s)"), w1_scales[:, rs, :].rearrange("p r s -> p (r s)"), w1_bf[:, rs, :, :].rearrange("p r s j -> p (r s j)"))
+        def quant_rows(codes, scales, values, first, count):
+            rows = slice(first, first + count)
+            quant(
+                codes[:, rows, :].rearrange("p a c -> p (a c)"),
+                scales[:, rows, :].rearrange("p a c -> p (a c)"),
+                values[:, rows, :, :].rearrange("p a c j -> p (a c j)"),
+            )
+
+        def quant_w1(first, count):
+            quant_rows(w1_codes, w1_scales, w1_bf, first, count)
 
         def quant_w2(first, count):
-            groups = slice(first, first + count)
-            quant(
-                w2_codes[:, groups, :].rearrange("s g m -> s (g m)"),
-                w2_scales[:, groups, :].rearrange("s g m -> s (g m)"),
-                w2_bf[:, groups, :, :].rearrange("s g m r -> s (g m r)"),
-            )
+            quant_rows(w2_codes, w2_scales, w2_bf, first, count)
 
         def quant_h(first, count):
-            units = slice(first, first + count)
-            quant(
-                h_codes[:, units, :].rearrange("s u n -> s (u n)"),
-                h_scales[:, units, :].rearrange("s u n -> s (u n)"),
-                h_bf[:, units, :, :].rearrange("s u n r -> s (u n r)"),
-            )
+            quant_rows(h_codes, h_scales, h_bf, first, count)
 
-        def first_layer(u, r):
-            c, g = ORDER[u]
-            rows = slice(ROWS * g, ROWS * (g + 1))
-            nc.tensor.matmul_mx(
-                out=(z_side if u == 0 and r >= 2 else z_ps[g])[:, r, :],
-                lhsT=w1_codes[rows, r, :].bitcast(FP8X4),
-                lhsT_scale=w1_scales[rows, r, :],
-                rhs=x_codes[c][rows, :].bitcast(FP8X4),
-                rhs_scale=x_scales[c][rows, :],
-                start=True,
-                stop=True,
-            )
+        def first_layer(first, count=1):
+            for r in range(PACK):
+                for u in range(first, first + count):
+                    c, g = divmod(u, G)
+                    rows = slice(ROWS * g, ROWS * (g + 1))
+                    nc.tensor.matmul_mx(
+                        out=(z_side if u == 0 and r >= 2 else z_ps[g])[:, r, :],
+                        lhsT=w1_codes[rows, r, :].bitcast(FP8X4),
+                        lhsT_scale=w1_scales[rows, r, :],
+                        rhs=x_codes[c][rows, :].bitcast(FP8X4),
+                        rhs_scale=x_scales[c][rows, :],
+                        start=True,
+                        stop=True,
+                    )
 
-        def second_layer(u, dst):
-            g = ORDER[u][1]
-            nc.tensor.matmul_mx(
-                out=dst,
-                lhsT=w2_codes[:, g, :].bitcast(FP8X4),
-                lhsT_scale=w2_scales[:, g, :],
-                rhs=h_codes[:, u, :].bitcast(FP8X4),
-                rhs_scale=h_scales[:, u, :],
-                start=True,
-                stop=True,
-            )
-
-        copies = {"V": nc.vector.tensor_copy, "S": nc.scalar.copy}
-
-        def piece_matmuls(i):
-            c0, chunks, g0, groups, bank = PIECES[i]
+        def second_layer(bank, c0, chunks, g0, groups, slot=0):
             for c in range(chunks):
                 for g in range(groups):
-                    second_layer(ORDER.index((c0 + c, g0 + g)), y_ps[bank][:, g * chunks + c, :])
+                    nc.tensor.matmul_mx(
+                        out=y_ps[bank][:, slot + g * chunks + c, :],
+                        lhsT=w2_codes[:, g0 + g, :].bitcast(FP8X4),
+                        lhsT_scale=w2_scales[:, g0 + g, :],
+                        rhs=h_codes[:, (c0 + c) * G + g0 + g, :].bitcast(FP8X4),
+                        rhs_scale=h_scales[:, (c0 + c) * G + g0 + g, :],
+                        start=True,
+                        stop=True,
+                    )
 
-        def piece_out(engine, i):
-            c0, chunks, g0, groups, bank = PIECES[i]
-            copies[engine](
-                out=y_sb[i][:].rearrange("m g n -> m (g n)"),
-                in_=y_ps[bank][:, 0 : groups * chunks, :].rearrange("m a n -> m (a n)"),
+        def store(copy, bank, c0, chunks, g0, groups, slot=0):
+            y_sb = sbuf("y_sb_c%d_g%d" % (c0, g0), [groups, chunks * COLS], F32, DMA_ALIGN)
+            copy(
+                out=y_sb[:].rearrange("m g n -> m (g n)"),
+                in_=y_ps[bank][:, slot : slot + groups * chunks, :].rearrange("m a n -> m (a n)"),
             )
-            out_piece = out[g0 : g0 + groups, :, c0 * COLS : (c0 + chunks) * COLS]
-            nc.sync.dma_start(out=out_piece.rearrange("g m n -> m g n"), in_=y_sb[i][:])
+            piece = out[g0 : g0 + groups, :, c0 * COLS : (c0 + chunks) * COLS]
+            nc.sync.dma_start(out=piece.rearrange("g m n -> m g n"), in_=y_sb[:])
+
+        y_sb = {}
+
+        def empty(copy, bank, slot, piece, c, chunks, g, groups):
+            c0, piece_chunks, g0, piece_groups = piece
+            if piece not in y_sb:
+                y_sb[piece] = sbuf("y_piece_c%d_g%d" % (c0, g0), [piece_groups, piece_chunks, COLS], F32, DMA_ALIGN)
+            dst = y_sb[piece][:, g - g0 : g - g0 + groups, c - c0 : c - c0 + chunks, :]
+            copy(out=dst, in_=y_ps[bank][:, slot : slot + groups * chunks, :].rearrange("m (g c) n -> m g c n", g=groups))
+
+        def put(piece):
+            c0, chunks, g0, groups = piece
+            dst = out[g0 : g0 + groups, :, c0 * COLS : (c0 + chunks) * COLS]
+            nc.sync.dma_start(out=dst.rearrange("g m n -> m g n"), in_=y_sb[piece][:].rearrange("m g c n -> m g (c n)"))
+
+        def halves_of_first():
+            return tanh_z[:, 0, :, :].rearrange("s n r -> s (n r)").rearrange("s (h n e) -> s h n e", h=2, e=2)
+
+        def tanh(u):
+            if u == 0:
+                for half, bank in enumerate((z_ps[0], z_side)):
+                    src = bank[:, 2 * half : 2 * half + 2, :].rearrange("s e n -> s n e")
+                    nc.scalar.activation(out=halves_of_first()[:, half, :, :], in_=src, func=ACT.Tanh)
+            else:
+                nc.scalar.activation(out=tanh_z[:, u, :, :], in_=z_ps[u % G][:].rearrange("s r n -> s n r"), func=ACT.Tanh)
 
         def mult(u, count=1):
-            g = ORDER[u][1]
-            scale = hs_sb[:, g : g + count, 0:PACK].unsqueeze(2).broadcast_to([P, count, COLS, PACK])
-            nc.vector.tensor_tensor(out=h_bf[:, u : u + count, :, :], in0=tanh_z[:, u : u + count, :, :], in1=scale, op=ALU.mult)
-
-        def mult_half(u, half):
-            cols = slice(half * COLS // 2, (half + 1) * COLS // 2)
-            scale = hs_sb[:, ORDER[u][1], 0:PACK].unsqueeze(1).broadcast_to([P, COLS // 2, PACK])
-            nc.vector.tensor_tensor(out=h_bf[:, u, cols, :], in0=tanh_z[:, u, cols, :], in1=scale, op=ALU.mult)
-
-        def mult_first():
-            halves = tanh_z[:, 0, :, :].rearrange("s n r -> s (n r)").rearrange("s (h n e) -> s n h e", h=2, e=2)
-            scale = hs_sb[:, ORDER[0][1], 0:PACK].rearrange("s (h e) -> s h e", h=2).unsqueeze(1).broadcast_to([P, COLS, 2, 2])
-            nc.vector.tensor_tensor(out=h_bf[:, 0, :, :].rearrange("s n (h e) -> s n h e", h=2), in0=halves, in1=scale, op=ALU.mult)
-
-        def unit_matmuls(u, count=1):
-            for r in range(PACK):
-                for unit in range(u, u + count):
-                    first_layer(unit, r)
-
-        jobs = {
-            "lay_x": lambda e, *a: lay_x(copies[e], *a),
-            "lay_w2": lambda e, *a: lay_w2(copies[e], *a),
-            "quant_x": quant_x,
-            "quant_w1": quant_w1,
-            "quant_w2": quant_w2,
-            "quant_h": quant_h,
-            "mm2": piece_matmuls,
-            "out": piece_out,
-            "mm1": unit_matmuls,
-            "mult": mult,
-            "mult_first": mult_first,
-            "mult_half": mult_half,
-        }
-
-        def run(steps):
-            for step in steps:
-                jobs[step[0]](*step[1:])
-
-        dst, src = dealt(0, W1_SPLIT)
-        nc.vector.tensor_copy(out=dst, in_=src)
-        dst, src = dealt(W1_SPLIT, P)
-        nc.scalar.activation(out=dst, in_=src, func=ACT.Copy)
-        run(HEAD)
-        for u in range(UNITS):
-            g = ORDER[u][1]
+            g = u % G
             if u == 0:
-                halves = tanh_z[:, 0, :, :].rearrange("s n r -> s (n r)").rearrange("s (h n e) -> s h n e", h=2, e=2)
-                for half, bank in enumerate((z_ps[g], z_side)):
-                    nc.scalar.activation(out=halves[:, half, :, :], in_=bank[:, 2 * half : 2 * half + 2, :].rearrange("s e n -> s n e"), func=ACT.Tanh)
+                scale = hs_sb[:, 0, 0:PACK].rearrange("s (h e) -> s h e", h=2).unsqueeze(1).broadcast_to([P, COLS, 2, 2])
+                dst = h_bf[:, 0, :, :].rearrange("s n (h e) -> s n h e", h=2)
+                nc.vector.tensor_tensor(out=dst, in0=halves_of_first().rearrange("s h n e -> s n h e"), in1=scale, op=ALU.mult)
             else:
-                nc.scalar.activation(out=tanh_z[:, u, :, :], in_=z_ps[g][:].rearrange("s r n -> s n r"), func=ACT.Tanh)
-            run(AFTER_TANH.get(u, []))
-            run(AFTER_MULT.get(u, [("mult", u)]))
-        run(TAIL)
+                scale = hs_sb[:, g : g + count, 0:PACK].unsqueeze(2).broadcast_to([P, count, COLS, PACK])
+                nc.vector.tensor_tensor(out=h_bf[:, u : u + count, :, :], in0=tanh_z[:, u : u + count, :, :], in1=scale, op=ALU.mult)
+
+        def scalar_first(out, in_):
+            nc.scalar.activation(out=out, in_=in_, func=ACT.Copy)
+
+        vector, scalar = nc.vector.tensor_copy, nc.scalar.copy
+
+        load_w1()
+        load_x(0, 1)
+        load_x(1, 1)
+        load_w2(0, 1)
+        load_w2(1, 1)
+        load_hs()
+        load_x(2, 2)
+        load_w2(2, 2)
+        deal_w1(vector, 0, 4, 0, 80)
+        deal_w1(scalar_first, 0, 4, 80, 128)
+        lay_x(vector, 0, 0, 96)
+        lay_x(scalar, 0, 96, 128)
+        quant_w1(0, 1)
+        quant_x(0)
+        quant_w1(1, 1)
+        quant_w1(2, 1)
+        quant_w1(3, 1)
+        lay_x(scalar, 1)
+        lay_w2(vector, 0)
+        quant_x(1)
+        lay_w2(vector, 1)
+        quant_w2(0, 2)
+        first_layer(0, 2)
+        first_layer(2, 2)
+        tanh(0)
+        first_layer(4)
+        mult(0)
+        tanh(1)
+        first_layer(5)
+        mult(1)
+        tanh(2)
+        first_layer(6)
+        mult(2)
+        lay_x(vector, 2, 64, 128)
+        tanh(3)
+        first_layer(7)
+        mult(3)
+        tanh(4)
+        lay_x(scalar, 2, 0, 64)
+        quant_x(2)
+        first_layer(8)
+        mult(4)
+        tanh(5)
+        first_layer(9)
+        mult(5)
+        quant_h(0, 4)
+        tanh(6)
+        first_layer(10)
+        tanh(7)
+        first_layer(11)
+        lay_x(scalar, 3)
+        mult(6, 2)
+        quant_x(3)
+        tanh(8)
+        first_layer(12)
+        mult(8)
+        quant_h(4, 4)
+        tanh(9)
+        first_layer(13)
+        tanh(10)
+        first_layer(14)
+        lay_w2(scalar, 2)
+        mult(9, 2)
+        tanh(11)
+        first_layer(15)
+        second_layer(0, 0, 2, 0, 2)
+        lay_w2(scalar, 3)
+        mult(11)
+        quant_w2(2, 2)
+        quant_h(8, 4)
+        tanh(12)
+        tanh(13)
+        mult(12, 2)
+        tanh(14)
+        store(scalar, 0, 0, 2, 0, 2)
+        mult(14)
+        quant_h(12, 2)
+        tanh(15)
+        mult(15)
+        quant_h(14, 1)
+        quant_h(15, 1)
+        second_layer(1, 0, 2, 2, 2)
+        store(scalar, 1, 0, 2, 2, 2)
+        second_layer(2, 2, 1, 0, 4)
+        store(scalar, 2, 2, 1, 0, 4)
+        second_layer(0, 3, 1, 0, 2)
+        store(scalar, 0, 3, 1, 0, 2)
+        second_layer(1, 3, 1, 2, 1)
+        store(scalar, 1, 3, 1, 2, 1)
+        second_layer(2, 3, 1, 3, 1)
+        store(scalar, 2, 3, 1, 3, 1)

@@ -186,6 +186,16 @@ def tile_rows_gmlp_tanh_kernel(tc, x, w1, hs, w2, out):
                 scale = hs_sb[:, g : g + count, 0:PACK].unsqueeze(2).broadcast_to([P, count, COLS, PACK])
                 nc.vector.tensor_tensor(out=h_bf[:, u : u + count, :, :], in0=tanh_z[:, u : u + count, :, :], in1=scale, op=ALU.mult)
 
+        def tanh_half(u, half):
+            cols = slice(half * COLS // 2, (half + 1) * COLS // 2)
+            src = z_ps[u % G][:, :, cols].rearrange("s r n -> s n r")
+            nc.scalar.activation(out=tanh_z[:, u, cols, :], in_=src, func=ACT.Tanh)
+
+        def mult_half(u, half):
+            cols = slice(half * COLS // 2, (half + 1) * COLS // 2)
+            scale = hs_sb[:, u % G, 0:PACK].unsqueeze(1).broadcast_to([P, COLS // 2, PACK])
+            nc.vector.tensor_tensor(out=h_bf[:, u, cols, :], in0=tanh_z[:, u, cols, :], in1=scale, op=ALU.mult)
+
         def scalar_first(out, in_):
             nc.scalar.activation(out=out, in_=in_, func=ACT.Copy)
 
@@ -199,10 +209,9 @@ def tile_rows_gmlp_tanh_kernel(tc, x, w1, hs, w2, out):
         load_hs()
         load_x(2, 2)
         load_w2(2, 2)
-        deal_w1(vector, 0, 4, 0, 80)
-        deal_w1(scalar_first, 0, 4, 80, 128)
-        lay_x(vector, 0, 0, 96)
-        lay_x(scalar, 0, 96, 128)
+        deal_w1(vector, 0, 2)
+        deal_w1(scalar_first, 2, 4)
+        lay_x(vector, 0)
         quant_w1(0, 1)
         quant_x(0)
         quant_w1(1, 1)
@@ -212,7 +221,8 @@ def tile_rows_gmlp_tanh_kernel(tc, x, w1, hs, w2, out):
         lay_w2(vector, 0)
         quant_x(1)
         lay_w2(vector, 1)
-        quant_w2(0, 2)
+        quant_w2(0, 1)
+        quant_w2(1, 1)
         first_layer(0, 2)
         first_layer(2, 2)
         tanh(0)

@@ -20,6 +20,7 @@ COLS = 128
 CHUNKS = N // COLS
 UNITS = G * CHUNKS
 HS_PITCH = 8
+WALK = 2
 ALIGN = 64
 
 DMA_ALIGN = 256
@@ -52,7 +53,7 @@ def tile_rows_gmlp_tanh_kernel(tc, x, w1, hs, w2, out):
         w2_bf = sbuf("w2_bf", [G, M, PACK], BF16)
         w2_codes = sbuf("w2_codes", [G, M], U32)
         w2_scales = sbuf("w2_scales", [G, M], U8)
-        tanh_z = sbuf("tanh_z", [UNITS, COLS, PACK], F32)
+        tanh_z = sbuf("tanh_z", [UNITS, PACK, COLS], F32)
         h_bf = sbuf("h_bf", [UNITS, COLS, PACK], BF16)
         h_codes = sbuf("h_codes", [UNITS, COLS], U32)
         h_scales = sbuf("h_scales", [UNITS, COLS], U8)
@@ -151,50 +152,23 @@ def tile_rows_gmlp_tanh_kernel(tc, x, w1, hs, w2, out):
             piece = out[g0 : g0 + groups, :, c0 * COLS : (c0 + chunks) * COLS]
             nc.sync.dma_start(out=piece.rearrange("g m n -> m g n"), in_=y_sb[:])
 
-        y_sb = {}
-
-        def empty(copy, bank, slot, piece, c, chunks, g, groups):
-            c0, piece_chunks, g0, piece_groups = piece
-            if piece not in y_sb:
-                y_sb[piece] = sbuf("y_piece_c%d_g%d" % (c0, g0), [piece_groups, piece_chunks, COLS], F32, DMA_ALIGN)
-            dst = y_sb[piece][:, g - g0 : g - g0 + groups, c - c0 : c - c0 + chunks, :]
-            copy(out=dst, in_=y_ps[bank][:, slot : slot + groups * chunks, :].rearrange("m (g c) n -> m g c n", g=groups))
-
-        def put(piece):
-            c0, chunks, g0, groups = piece
-            dst = out[g0 : g0 + groups, :, c0 * COLS : (c0 + chunks) * COLS]
-            nc.sync.dma_start(out=dst.rearrange("g m n -> m g n"), in_=y_sb[piece][:].rearrange("m g c n -> m g (c n)"))
-
-        def halves_of_first():
-            return tanh_z[:, 0, :, :].rearrange("s n r -> s (n r)").rearrange("s (h n e) -> s h n e", h=2, e=2)
-
         def tanh(u):
             if u == 0:
                 for half, bank in enumerate((z_ps[0], z_side)):
-                    src = bank[:, 2 * half : 2 * half + 2, :].rearrange("s e n -> s n e")
-                    nc.scalar.activation(out=halves_of_first()[:, half, :, :], in_=src, func=ACT.Tanh)
+                    rs = slice(2 * half, 2 * half + 2)
+                    nc.scalar.activation(out=tanh_z[:, 0, rs, :], in_=bank[:, rs, :], func=ACT.Tanh)
             else:
-                nc.scalar.activation(out=tanh_z[:, u, :, :], in_=z_ps[u % G][:].rearrange("s r n -> s n r"), func=ACT.Tanh)
+                nc.scalar.activation(out=tanh_z[:, u, :, :], in_=z_ps[u % G][:], func=ACT.Tanh)
 
-        def mult(u, count=1):
-            g = u % G
-            if u == 0:
-                scale = hs_sb[:, 0, 0:PACK].rearrange("s (h e) -> s h e", h=2).unsqueeze(1).broadcast_to([P, COLS, 2, 2])
-                dst = h_bf[:, 0, :, :].rearrange("s n (h e) -> s n h e", h=2)
-                nc.vector.tensor_tensor(out=dst, in0=halves_of_first().rearrange("s h n e -> s n h e"), in1=scale, op=ALU.mult)
-            else:
-                scale = hs_sb[:, g : g + count, 0:PACK].unsqueeze(2).broadcast_to([P, count, COLS, PACK])
-                nc.vector.tensor_tensor(out=h_bf[:, u : u + count, :, :], in0=tanh_z[:, u : u + count, :, :], in1=scale, op=ALU.mult)
-
-        def tanh_half(u, half):
-            cols = slice(half * COLS // 2, (half + 1) * COLS // 2)
-            src = z_ps[u % G][:, :, cols].rearrange("s r n -> s n r")
-            nc.scalar.activation(out=tanh_z[:, u, cols, :], in_=src, func=ACT.Tanh)
-
-        def mult_half(u, half):
-            cols = slice(half * COLS // 2, (half + 1) * COLS // 2)
-            scale = hs_sb[:, u % G, 0:PACK].unsqueeze(1).broadcast_to([P, COLS // 2, PACK])
-            nc.vector.tensor_tensor(out=h_bf[:, u, cols, :], in0=tanh_z[:, u, cols, :], in1=scale, op=ALU.mult)
+        def mult(first, count=1):
+            for u in range(first, first + count):
+                scale = hs_sb[:, u % G, 0:PACK].unsqueeze(1).unsqueeze(3).broadcast_to([P, COLS // WALK, PACK, WALK])
+                nc.vector.tensor_tensor(
+                    out=h_bf[:, u, :, :].rearrange("s (c i) r -> s c r i", i=WALK),
+                    in0=tanh_z[:, u, :, :].rearrange("s r (c i) -> s c r i", i=WALK),
+                    in1=scale,
+                    op=ALU.mult,
+                )
 
         def scalar_first(out, in_):
             nc.scalar.activation(out=out, in_=in_, func=ACT.Copy)

@@ -208,46 +208,51 @@ def tile_rows_gmlp_tanh_kernel(tc, x, w1, hs, w2, out):
         tanh(2)
         first_layer(6)
         mult(2)
-        lay_x(vector, 2, 64, 128)
+        quant_h(0, 2)
         tanh(3)
         first_layer(7)
         mult(3)
         tanh(4)
-        lay_x(scalar, 2, 0, 64)
+        lay_x(scalar, 2)
+        mult(4)
         quant_x(2)
         first_layer(8)
-        mult(4)
+        quant_h(2, 2)
         tanh(5)
         first_layer(9)
         mult(5)
-        quant_h(0, 4)
         tanh(6)
         first_layer(10)
+        mult(6)
+        quant_h(4, 2)
         tanh(7)
         first_layer(11)
         lay_x(scalar, 3)
-        mult(6, 2)
+        mult(7)
         quant_x(3)
         tanh(8)
         first_layer(12)
         mult(8)
-        quant_h(4, 4)
+        quant_h(6, 2)
         tanh(9)
         first_layer(13)
+        mult(9)
         tanh(10)
         first_layer(14)
         lay_w2(scalar, 2)
-        mult(9, 2)
+        mult(10)
+        quant_h(8, 2)
         tanh(11)
         first_layer(15)
         second_layer(0, 0, 2, 0, 2)
-        lay_w2(scalar, 3)
         mult(11)
-        quant_w2(2, 2)
-        quant_h(8, 4)
         tanh(12)
+        lay_w2(scalar, 3)
+        mult(12)
+        quant_w2(2, 2)
+        quant_h(10, 2)
         tanh(13)
-        mult(12, 2)
+        mult(13)
         tanh(14)
         store(scalar, 0, 0, 2, 0, 2)
         mult(14)

@@ -206,45 +206,40 @@ def tile_rows_gmlp_tanh_kernel(tc, x, w1, hs, w2, out):
         first_layer(5)
         mult(1)
         tanh(2)
-        first_layer(6)
         mult(2)
         quant_h(0, 2)
         tanh(3)
-        first_layer(7)
+        first_layer(6, 2)
         mult(3)
         tanh(4)
         lay_x(scalar, 2)
         mult(4)
         quant_x(2)
-        first_layer(8)
         quant_h(2, 2)
         tanh(5)
-        first_layer(9)
+        first_layer(8, 2)
         mult(5)
         tanh(6)
-        first_layer(10)
         mult(6)
         quant_h(4, 2)
         tanh(7)
-        first_layer(11)
+        first_layer(10, 2)
+        second_layer(0, 0, 2, 0, 2)
         lay_x(scalar, 3)
         mult(7)
         quant_x(3)
         tanh(8)
-        first_layer(12)
         mult(8)
         quant_h(6, 2)
         tanh(9)
-        first_layer(13)
+        first_layer(12, 2)
         mult(9)
         tanh(10)
-        first_layer(14)
         lay_w2(scalar, 2)
         mult(10)
         quant_h(8, 2)
         tanh(11)
-        first_layer(15)
-        second_layer(0, 0, 2, 0, 2)
+        first_layer(14, 2)
         mult(11)
         tanh(12)
         lay_w2(scalar, 3)

@@ -17,6 +17,7 @@ P = 128
 PACK = 4
 ROWS = D // PACK
 COLS = 128
+HALF = COLS // 2
 CHUNKS = N // COLS
 UNITS = G * CHUNKS
 HS_PITCH = 8
@@ -53,7 +54,8 @@ def tile_rows_gmlp_tanh_kernel(tc, x, w1, hs, w2, out):
         w2_bf = sbuf("w2_bf", [G, M, PACK], BF16)
         w2_codes = sbuf("w2_codes", [G, M], U32)
         w2_scales = sbuf("w2_scales", [G, M], U8)
-        tanh_z = sbuf("tanh_z", [UNITS, PACK, COLS], F32)
+        tanh_z = sbuf("tanh_z", [UNITS - 1, PACK, COLS], F32)
+        tanh_last = [sbuf("tanh_last%d" % half, [HALF, PACK], F32) for half in range(2)]
         h_bf = sbuf("h_bf", [UNITS, COLS, PACK], BF16)
         h_codes = sbuf("h_codes", [UNITS, COLS], U32)
         h_scales = sbuf("h_scales", [UNITS, COLS], U8)
@@ -170,6 +172,26 @@ def tile_rows_gmlp_tanh_kernel(tc, x, w1, hs, w2, out):
                     op=ALU.mult,
                 )
 
+        def half_cols(half):
+            return slice(half * HALF, (half + 1) * HALF)
+
+        def tanh_half(u, half):
+            src = z_ps[u % G][:, :, half_cols(half)].rearrange("s r n -> s n r")
+            nc.scalar.activation(out=tanh_last[half][:], in_=src, func=ACT.Tanh)
+
+        def mult_half(u, half):
+            scale = hs_sb[:, u % G, 0:PACK].unsqueeze(1).broadcast_to([P, HALF, PACK])
+            nc.vector.tensor_tensor(out=h_bf[:, u, half_cols(half), :], in0=tanh_last[half][:], in1=scale, op=ALU.mult)
+
+        def quant_h_half(u, half):
+            cols = half_cols(half)
+            quant(h_codes[:, u, cols], h_scales[:, u, cols], h_bf[:, u, cols, :].rearrange("s n r -> s (n r)"))
+
+        def lay_w2_pair(copy, g):
+            dst = w2_bf[:, g : g + 2, :, :].rearrange("s g (c i) r -> s g c r i", i=4)
+            src = w2_raw[:, g : g + 2, :].rearrange("s g (r c i) -> s g c r i", r=PACK, i=4)
+            copy(out=dst, in_=src)
+
         def scalar_first(out, in_):
             nc.scalar.activation(out=out, in_=in_, func=ACT.Copy)
 
@@ -205,57 +227,65 @@ def tile_rows_gmlp_tanh_kernel(tc, x, w1, hs, w2, out):
         tanh(1)
         first_layer(5)
         mult(1)
+        quant_h(0, 1)
         tanh(2)
+        first_layer(6)
         mult(2)
-        quant_h(0, 2)
         tanh(3)
-        first_layer(6, 2)
+        first_layer(7)
         mult(3)
+        quant_h(1, 2)
         tanh(4)
         lay_x(scalar, 2)
         mult(4)
         quant_x(2)
-        quant_h(2, 2)
+        first_layer(8)
         tanh(5)
-        first_layer(8, 2)
+        first_layer(9)
         mult(5)
+        quant_h(3, 2)
         tanh(6)
+        first_layer(10)
         mult(6)
-        quant_h(4, 2)
         tanh(7)
-        first_layer(10, 2)
-        second_layer(0, 0, 2, 0, 2)
+        first_layer(11)
         lay_x(scalar, 3)
         mult(7)
+        quant_h(5, 2)
         quant_x(3)
         tanh(8)
+        first_layer(12)
         mult(8)
-        quant_h(6, 2)
         tanh(9)
-        first_layer(12, 2)
+        first_layer(13)
         mult(9)
+        quant_h(7, 2)
         tanh(10)
-        lay_w2(scalar, 2)
+        first_layer(14)
         mult(10)
-        quant_h(8, 2)
         tanh(11)
-        first_layer(14, 2)
+        first_layer(15)
+        second_layer(0, 0, 2, 0, 2)
+        lay_w2_pair(scalar, 2)
         mult(11)
-        tanh(12)
-        lay_w2(scalar, 3)
-        mult(12)
+        quant_h(9, 2)
         quant_w2(2, 2)
-        quant_h(10, 2)
+        tanh(12)
+        mult(12)
         tanh(13)
         mult(13)
+        quant_h(11, 2)
         tanh(14)
         store(scalar, 0, 0, 2, 0, 2)
         mult(14)
-        quant_h(12, 2)
-        tanh(15)
-        mult(15)
+        quant_h(13, 1)
+        tanh_half(15, 0)
+        tanh_half(15, 1)
+        mult_half(15, 0)
+        mult_half(15, 1)
         quant_h(14, 1)
-        quant_h(15, 1)
+        quant_h_half(15, 0)
+        quant_h_half(15, 1)
         second_layer(1, 0, 2, 2, 2)
         store(scalar, 1, 0, 2, 2, 2)
         second_layer(2, 2, 1, 0, 4)

@@ -183,10 +183,6 @@ def tile_rows_gmlp_tanh_kernel(tc, x, w1, hs, w2, out):
             scale = hs_sb[:, u % G, 0:PACK].unsqueeze(1).broadcast_to([P, HALF, PACK])
             nc.vector.tensor_tensor(out=h_bf[:, u, half_cols(half), :], in0=tanh_last[half][:], in1=scale, op=ALU.mult)
 
-        def quant_h_half(u, half):
-            cols = half_cols(half)
-            quant(h_codes[:, u, cols], h_scales[:, u, cols], h_bf[:, u, cols, :].rearrange("s n r -> s (n r)"))
-
         def lay_w2_pair(copy, g):
             dst = w2_bf[:, g : g + 2, :, :].rearrange("s g (c i) r -> s g c r i", i=4)
             src = w2_raw[:, g : g + 2, :].rearrange("s g (r c i) -> s g c r i", r=PACK, i=4)
@@ -284,8 +280,7 @@ def tile_rows_gmlp_tanh_kernel(tc, x, w1, hs, w2, out):
         mult_half(15, 0)
         mult_half(15, 1)
         quant_h(14, 1)
-        quant_h_half(15, 0)
-        quant_h_half(15, 1)
+        quant_h(15, 1)
         second_layer(1, 0, 2, 2, 2)
         store(scalar, 1, 0, 2, 2, 2)
         second_layer(2, 2, 1, 0, 4)

@@ -239,7 +239,6 @@ def tile_rows_gmlp_tanh_kernel(tc, x, w1, hs, w2, out):
         tanh(5)
         first_layer(9)
         mult(5)
-        quant_h(3, 2)
         tanh(6)
         first_layer(10)
         mult(6)
@@ -247,7 +246,7 @@ def tile_rows_gmlp_tanh_kernel(tc, x, w1, hs, w2, out):
         first_layer(11)
         lay_x(scalar, 3)
         mult(7)
-        quant_h(5, 2)
+        quant_h(3, 4)
         quant_x(3)
         tanh(8)
         first_layer(12)
@@ -255,7 +254,6 @@ def tile_rows_gmlp_tanh_kernel(tc, x, w1, hs, w2, out):
         tanh(9)
         first_layer(13)
         mult(9)
-        quant_h(7, 2)
         tanh(10)
         first_layer(14)
         mult(10)
@@ -264,7 +262,7 @@ def tile_rows_gmlp_tanh_kernel(tc, x, w1, hs, w2, out):
         second_layer(0, 0, 2, 0, 2)
         lay_w2_pair(scalar, 2)
         mult(11)
-        quant_h(9, 2)
+        quant_h(7, 4)
         quant_w2(2, 2)
         tanh(12)
         mult(12)

from contextlib import ExitStack

import concourse.mybir as mybir

G, D, K, M, N = 4, 128, 512, 128, 512
FLOPS = 2 * G * D * K * N + 2 * G * K * M * N

F32 = mybir.dt.float32
BF16 = mybir.dt.bfloat16
U32 = mybir.dt.uint32
U8 = mybir.dt.uint8
FP8X4 = mybir.dt.float8_e4m3fn_x4
ACT = mybir.ActivationFunctionType
ALU = mybir.AluOpType

P = 128
PACK = 4
ROWS = D // PACK
COLS = 128
HALF = COLS // 2
CHUNKS = N // COLS
UNITS = G * CHUNKS
HS_PITCH = 8
WALK = 2
ALIGN = 64

DMA_ALIGN = 256


def tile_rows_gmlp_tanh_kernel(tc, x, w1, hs, w2, out):
    nc = tc.nc
    with ExitStack() as ctx:
        sb = ctx.enter_context(tc.tile_pool(name="sb", bufs=1))
        ps = ctx.enter_context(tc.psum_pool(name="ps", bufs=1))
        ctx.enter_context(tc.manual_schedule())

        def sbuf(name, shape, dtype, align=ALIGN):
            return sb.tile([P] + shape, dtype, name=name, align_bytes=align)

        x_hbm = x.flatten_outer_dims().rearrange("(p j) n -> p j n", j=PACK)
        w1_hbm = w1.flatten_outer_dims().rearrange("(p j) k -> p j k", j=PACK)
        w2_hbm = w2.rearrange("g (s r) m -> s g (r m)", r=PACK)
        hs_hbm = hs.rearrange("g (s r) o -> s g (r o)", r=PACK)
        w1_raw = sbuf("w1_raw", [PACK, K], F32, DMA_ALIGN)
        w2_raw = sbuf("w2_raw", [G, PACK * M], F32, DMA_ALIGN)
        hs_sb = sbuf("hs_sb", [G, HS_PITCH], F32, DMA_ALIGN)
        x_raw = {}
        x_bf = [sbuf("x_bf%d" % c, [COLS, PACK], BF16) for c in range(CHUNKS)]
        x_codes = [sbuf("x_codes%d" % c, [COLS], U32) for c in range(CHUNKS)]
        x_scales = [sbuf("x_scales%d" % c, [COLS], U8) for c in range(CHUNKS)]
        w1_bf = sbuf("w1_bf", [PACK, P, PACK], BF16)
        w1_codes = sbuf("w1_codes", [PACK, P], U32)
        w1_scales = sbuf("w1_scales", [PACK, P], U8)
        w2_bf = sbuf("w2_bf", [G, M, PACK], BF16)
        w2_codes = sbuf("w2_codes", [G, M], U32)
        w2_scales = sbuf("w2_scales", [G, M], U8)
        tanh_z = sbuf("tanh_z", [UNITS - 1, PACK, COLS], F32)
        tanh_last = [sbuf("tanh_last%d" % half, [HALF, PACK], F32) for half in range(2)]
        h_bf = sbuf("h_bf", [UNITS, COLS, PACK], BF16)
        h_codes = sbuf("h_codes", [UNITS, COLS], U32)
        h_scales = sbuf("h_scales", [UNITS, COLS], U8)
        z_ps = [ps.tile([P, PACK, COLS], F32, name="z_ps%d" % g) for g in range(G)]
        z_side = ps.tile([P, PACK, COLS], F32, name="z_side")
        y_ps = [ps.tile([P, PACK, COLS], F32, name="y_ps%d" % b) for b in range(3)]

        def load_w1():
            nc.sync.dma_start(out=w1_raw[:], in_=w1_hbm)

        def load_x(first, count):
            raw = sbuf("x_raw%d" % first, [PACK, count * COLS], F32, DMA_ALIGN)
            nc.sync.dma_start(out=raw[:], in_=x_hbm[:, :, first * COLS : (first + count) * COLS])
            for c in range(count):
                x_raw[first + c] = raw[:, :, c * COLS : (c + 1) * COLS]

        def load_w2(first, count):
            groups = slice(first, first + count)
            nc.sync.dma_start(out=w2_raw[:, groups, :], in_=w2_hbm[:, groups, :])

        def load_hs(first=0, count=G):
            groups = slice(first, first + count)
            nc.sync.dma_start(out=hs_sb[:, groups, 0:PACK], in_=hs_hbm[:, groups, :])

        def lay(copy, dst, src):
            copy(out=dst.rearrange("p (c i) j -> p c j i", i=4), in_=src.rearrange("p j (c i) -> p c j i", i=4))

        def lay_x(copy, c, n0=0, n1=COLS):
            lay(copy, x_bf[c][:, n0:n1, :], x_raw[c][:, :, n0:n1])

        def lay_w2(copy, g, m0=0, m1=M):
            lay(copy, w2_bf[:, g, m0:m1, :], w2_raw[:, g, :].rearrange("s (r m) -> s r m", r=PACK)[:, :, m0:m1])

        def deal_w1(copy, r0, r1, s0=0, s1=P):
            dst = w1_bf[:, r0:r1, s0:s1, :].rearrange("p r s j -> p s j r")
            src = w1_raw[:].rearrange("p j (s r) -> p s j r", r=PACK)[:, s0:s1, :, r0:r1]
            copy(out=dst, in_=src)

        def quant(codes, scales, values):
            nc.vector.quantize_mx(out=codes.bitcast(FP8X4), scales=scales, in_=values)

        def quant_x(c):
            quant(x_codes[c][:], x_scales[c][:], x_bf[c][:].rearrange("p n j -> p (n j)"))

        def quant_rows(codes, scales, values, first, count):
            rows = slice(first, first + count)
            quant(
                codes[:, rows, :].rearrange("p a c -> p (a c)"),
                scales[:, rows, :].rearrange("p a c -> p (a c)"),
                values[:, rows, :, :].rearrange("p a c j -> p (a c j)"),
            )

        def quant_w1(first, count):
            quant_rows(w1_codes, w1_scales, w1_bf, first, count)

        def quant_w2(first, count):
            quant_rows(w2_codes, w2_scales, w2_bf, first, count)

        def quant_h(first, count):
            quant_rows(h_codes, h_scales, h_bf, first, count)

        def first_layer(first, count=1):
            for r in range(PACK):
                for u in range(first, first + count):
                    c, g = divmod(u, G)
                    rows = slice(ROWS * g, ROWS * (g + 1))
                    nc.tensor.matmul_mx(
                        out=(z_side if u == 0 and r >= 2 else z_ps[g])[:, r, :],
                        lhsT=w1_codes[rows, r, :].bitcast(FP8X4),
                        lhsT_scale=w1_scales[rows, r, :],
                        rhs=x_codes[c][rows, :].bitcast(FP8X4),
                        rhs_scale=x_scales[c][rows, :],
                        start=True,
                        stop=True,
                    )

        def second_layer(bank, c0, chunks, g0, groups, slot=0):
            for c in range(chunks):
                for g in range(groups):
                    nc.tensor.matmul_mx(
                        out=y_ps[bank][:, slot + g * chunks + c, :],
                        lhsT=w2_codes[:, g0 + g, :].bitcast(FP8X4),
                        lhsT_scale=w2_scales[:, g0 + g, :],
                        rhs=h_codes[:, (c0 + c) * G + g0 + g, :].bitcast(FP8X4),
                        rhs_scale=h_scales[:, (c0 + c) * G + g0 + g, :],
                        start=True,
                        stop=True,
                    )

        def store(copy, bank, c0, chunks, g0, groups, slot=0):
            y_sb = sbuf("y_sb_c%d_g%d" % (c0, g0), [groups, chunks * COLS], F32, DMA_ALIGN)
            copy(
                out=y_sb[:].rearrange("m g n -> m (g n)"),
                in_=y_ps[bank][:, slot : slot + groups * chunks, :].rearrange("m a n -> m (a n)"),
            )
            piece = out[g0 : g0 + groups, :, c0 * COLS : (c0 + chunks) * COLS]
            nc.sync.dma_start(out=piece.rearrange("g m n -> m g n"), in_=y_sb[:])

        def tanh(u):
            if u == 0:
                for half, bank in enumerate((z_ps[0], z_side)):
                    rs = slice(2 * half, 2 * half + 2)
                    nc.scalar.activation(out=tanh_z[:, 0, rs, :], in_=bank[:, rs, :], func=ACT.Tanh)
            else:
                nc.scalar.activation(out=tanh_z[:, u, :, :], in_=z_ps[u % G][:], func=ACT.Tanh)

        def mult(first, count=1):
            for u in range(first, first + count):
                scale = hs_sb[:, u % G, 0:PACK].unsqueeze(1).unsqueeze(3).broadcast_to([P, COLS // WALK, PACK, WALK])
                nc.vector.tensor_tensor(
                    out=h_bf[:, u, :, :].rearrange("s (c i) r -> s c r i", i=WALK),
                    in0=tanh_z[:, u, :, :].rearrange("s r (c i) -> s c r i", i=WALK),
                    in1=scale,
                    op=ALU.mult,
                )

        def half_cols(half):
            return slice(half * HALF, (half + 1) * HALF)

        def tanh_half(u, half):
            src = z_ps[u % G][:, :, half_cols(half)].rearrange("s r n -> s n r")
            nc.scalar.activation(out=tanh_last[half][:], in_=src, func=ACT.Tanh)

        def mult_half(u, half):
            scale = hs_sb[:, u % G, 0:PACK].unsqueeze(1).broadcast_to([P, HALF, PACK])
            nc.vector.tensor_tensor(out=h_bf[:, u, half_cols(half), :], in0=tanh_last[half][:], in1=scale, op=ALU.mult)

        def lay_w2_pair(copy, g):
            dst = w2_bf[:, g : g + 2, :, :].rearrange("s g (c i) r -> s g c r i", i=4)
            src = w2_raw[:, g : g + 2, :].rearrange("s g (r c i) -> s g c r i", r=PACK, i=4)
            copy(out=dst, in_=src)

        def scalar_first(out, in_):
            nc.scalar.activation(out=out, in_=in_, func=ACT.Copy)

        vector, scalar = nc.vector.tensor_copy, nc.scalar.copy

        load_w1()
        load_x(0, 1)
        load_x(1, 1)
        load_w2(0, 1)
        load_w2(1, 1)
        load_hs()
        load_x(2, 2)
        load_w2(2, 2)
        deal_w1(vector, 0, 2)
        deal_w1(scalar_first, 2, 4)
        lay_x(vector, 0)
        quant_w1(0, 1)
        quant_x(0)
        quant_w1(1, 1)
        quant_w1(2, 1)
        quant_w1(3, 1)
        lay_x(scalar, 1)
        lay_w2(vector, 0)
        quant_x(1)
        lay_w2(vector, 1)
        quant_w2(0, 1)
        quant_w2(1, 1)
        first_layer(0, 2)
        first_layer(2, 2)
        tanh(0)
        first_layer(4)
        mult(0)
        tanh(1)
        first_layer(5)
        mult(1)
        quant_h(0, 1)
        tanh(2)
        first_layer(6)
        mult(2)
        tanh(3)
        first_layer(7)
        mult(3)
        quant_h(1, 2)
        tanh(4)
        lay_x(scalar, 2)
        mult(4)
        quant_x(2)
        first_layer(8)
        tanh(5)
        first_layer(9)
        mult(5)
        tanh(6)
        first_layer(10)
        mult(6)
        tanh(7)
        first_layer(11)
        lay_x(scalar, 3)
        mult(7)
        quant_h(3, 4)
        quant_x(3)
        tanh(8)
        first_layer(12)
        mult(8)
        tanh(9)
        first_layer(13)
        mult(9)
        tanh(10)
        first_layer(14)
        mult(10)
        tanh(11)
        first_layer(15)
        second_layer(0, 0, 2, 0, 2)
        lay_w2_pair(scalar, 2)
        mult(11)
        quant_h(7, 4)
        quant_w2(2, 2)
        tanh(12)
        mult(12)
        tanh(13)
        mult(13)
        quant_h(11, 2)
        tanh(14)
        store(scalar, 0, 0, 2, 0, 2)
        mult(14)
        quant_h(13, 1)
        tanh_half(15, 0)
        tanh_half(15, 1)
        mult_half(15, 0)
        mult_half(15, 1)
        quant_h(14, 1)
        quant_h(15, 1)
        second_layer(1, 0, 2, 2, 2)
        store(scalar, 1, 0, 2, 2, 2)
        second_layer(2, 2, 1, 0, 4)
        store(scalar, 2, 2, 1, 0, 4)
        second_layer(0, 3, 1, 0, 2)
        store(scalar, 0, 3, 1, 0, 2)
        second_layer(1, 3, 1, 2, 1)
        store(scalar, 1, 3, 1, 2, 1)
        second_layer(2, 3, 1, 3, 1)
        store(scalar, 2, 3, 1, 3, 1)
